import numpy as np, ml_dtypes
CORES = [1,5,17,21,33,37,49,53]
N = 8
import mx_ref
BF = ml_dtypes.bfloat16
def entries(a):
    return np.ascontiguousarray(a.T).reshape(-1)
def table(e):
    return np.ascontiguousarray(np.reshape(e, (-1, 16)).T).astype(np.int32)
def pick(q, e):
    c = np.concatenate([q[0].reshape(128, -1, 4), np.zeros((128, 1, 4), np.uint8)], axis=1); s = np.concatenate([q[1], np.ones((16, 1), np.uint8)], axis=1)
    return (np.ascontiguousarray(c[:, e].reshape(128, -1)), np.ascontiguousarray(s[:, e]))
def join(*qs):
    return (np.concatenate([q[0] for q in qs], axis=1), np.concatenate([q[1] for q in qs], axis=1))
def put(q, e, v):
    c, s = q[0].reshape(128, -1, 4).copy(), q[1].copy(); c[:, e] = v[0].reshape(128, -1, 4); s[:, e] = v[1]
    return (c.reshape(128, -1), s)
def pk(c, s):
    return (np.ascontiguousarray(c), mx_ref.live(s))
def emit(q):
    return q[0], q[1]
def decode(q):
    o = []
    for b in range(4):
        e = np.zeros((128, 128, 4), np.float32); e[np.arange(128), np.arange(128), b] = 1
        o.append(mx_ref.matmul(mx_ref.quantize(e.reshape(128, 512).astype(BF)), q))
    return np.stack(o, axis=2).reshape(128, -1)
def cut(t, i, w=512):
    return t[:, w * i:w * i + w]
def f(rng, *shape):
    return mx_ref.flush((rng.standard_normal(shape, dtype=np.float32) * np.exp2(rng.integers(-2, 3, shape[:-1] + (1,)))).astype(BF))
def wide(rng, *shape, cols=0):
    v = rng.standard_normal(shape, dtype=np.float32) * np.exp2(rng.integers(-12, 13, shape)).astype(np.float32)
    if cols: v *= np.repeat(np.exp2(rng.integers(-cols, cols + 1, shape[:-2] + (1, shape[-1] // 4))) * (rng.random(shape[:-2] + (1, shape[-1] // 4)) > 0.0625), 4, axis=-1).astype(np.float32)
    return mx_ref.flush(v.astype(BF))
P, S, K, R, B, M, O = 256, 32, 32, 3, 48, 4, 2
def big(v):
    v = np.array(v).astype(np.float32)
    v[np.abs(v) < np.float32(2.0 ** -16)] = 0
    return v.astype(BF)
def link(adj, a, b):
    a, b = int(a), int(b)
    if a != b and len(adj[a]) < M and len(adj[b]) < M and b not in adj[a]:
        adj[a].append(b)
        adj[b].append(a)
def inner(rng, adj, e):
    for t in range(2 * M):
        a = rng.permutation(e)
        for i in range(0, a.size - 1, 2): link(adj, a[i], a[i + 1])
def across(rng, adj, ranks):
    for r in ranks:
        for q in ranks:
            if r < q:
                a, c = P * r + rng.permutation(P), P * q + rng.permutation(P)
                n = int(rng.integers(B // 2, B + 1))
                for i in range(n):
                    link(adj, a[i], c[i])
                    if i % 3 == 0: link(adj, a[i], c[(i + 1) % n])
def graph(rng):
    adj = [[] for a in range(N * P)]
    across(rng, adj, range(N))
    for r in range(N): inner(rng, adj, np.arange(P * r, P * r + P))
    return adj
def seeds(rng):
    return np.stack([rng.permutation(P)[:S] for r in range(N)])
def lists(rng, adj, s, late=False):
    at = np.argsort(rng.random((N * P, M)), axis=1)
    seed = np.zeros(N * P, bool)
    for r in range(N): seed[P * r + s[r]] = True
    n = np.full((N, M, P), -1)
    for a in range(N * P):
        k, e = at[a, :len(adj[a])], adj[a]
        if late: k, e = np.sort(k), sorted(e, key=lambda c: bool(seed[c]))
        for i, c in zip(k, e): n[a // P, i, a % P] = c
    return {"nb": np.stack([table(v.reshape(-1)) for v in n]), "sd": np.stack([table(v) for v in s])}
def plain(rng):
    return {"x": big(f(rng, N, 128, 4 * P)), "w": f(rng, N, 128, 512 * O)}
def setup_inputs(rng):
    return {**plain(rng), **lists(rng, graph(rng), seeds(rng))}
def setup_inputs_caps(rng):
    o = np.stack([rng.permutation(P) for r in range(N)])
    adj = [[] for a in range(N * P)]
    dense = int(rng.integers(0, N))
    for r in range(N):
        q = (r + 1) % N
        if r == dense:
            a = P * r + np.concatenate([o[r, S:S + K], o[r, K + B:2 * B]])
            c = P * q + np.concatenate([o[q, :S // 2], rng.permutation(np.concatenate([o[q, S // 2:S], o[q, S + K:K + B]]))])
            for i in range(B):
                for j in range(i - i % M, min(i - i % M + M, B)): link(adj, a[i], c[j])
        else:
            for i in range(K):
                link(adj, P * r + o[r, S + i], P * q + o[q, i])
                link(adj, P * r + o[r, S + i], P * q + o[q, S + K + i % (B - S)])
    for r in range(N): inner(rng, adj, P * r + o[r, S:])
    return {**plain(rng), **lists(rng, adj, o[:, :S])}
def setup_inputs_few(rng):
    adj, s, o, n, m = [[] for a in range(N * P)], seeds(rng), rng.permutation(N), K // 2 - 1, S // 2
    some, rest = int(o[1]), sorted(o[2:].tolist())
    ends = np.unique([0, 127, P - 1])
    s[some] = rng.permutation(np.setdiff1d(np.arange(P), ends))[:S]
    free, at, zero = rng.permutation(np.setdiff1d(np.arange(P), np.concatenate([s[some], ends]))), 0, []
    for i in range(K // 2):
        end = s[some, i]
        for t in range(1 + i % R):
            link(adj, P * some + end, P * some + free[at])
            end = free[at]
            at += 1
        if i < K // 4: zero.append(int(end))
    idle = np.sort(free[at:])
    lone = np.concatenate([ends, idle[:n - ends.size]])
    idle = rng.permutation(idle[n - ends.size:])
    for i in range(idle.size): link(adj, P * some + idle[i - 1], P * some + idle[i])
    for r in rest[:2]:
        g, e = rng.permutation(P // 8)[:n], P // 8 + rng.permutation(P // 8)[:m]
        s[r] = rng.permutation(np.setdiff1d(np.arange(P), np.concatenate([g, e])))[:S]
        high = rng.permutation(np.setdiff1d(np.arange(3 * P // 8, P), s[r]))
        for i in range(K): link(adj, P * r + s[r, i], P * r + high[i])
        for i in range(n):
            link(adj, P * r + s[r, i], P * r + g[i])
            link(adj, P * some + lone[i], P * r + g[i])
        for i in range(m):
            link(adj, P * r + s[r, n + i], P * r + e[i])
            link(adj, P * some + s[some, m + i], P * r + e[i])
    across(rng, adj, rest)
    for r in rest: inner(rng, adj, np.arange(P * r, P * r + P))
    sign = np.ones(N)
    sign[rest[::2]] = -0.75
    j = np.arange(P)
    v = f(rng, N, 128, 4 * P).astype(np.float32).reshape(N, 128, P, 4)
    v[:, :64] = 0
    for r in range(N):
        on = np.isin(j, s[r])
        v[r][64:96][:, ~on] = 0
        v[r][96:][:, on] = 0
        v[r, 0, :, 0] = 1024.0 * np.where(on, 1.0, sign[r])
        v[r, 40, :, 0] = np.where(on, rng.integers(1, 3, P), 0.125 * (8 * j // P))
    for r in rest[:2]: v[r, 40, s[r, n:n + m], 0] = 2.0
    v[some, 40, s[some, m:], 0] = 1.0
    v[some, 0, lone, 0] = 4096.0
    v[some][:, zero] = 0
    return {**plain(rng), "x": big(v.reshape(N, 128, 4 * P)), **lists(rng, adj, s)}
def setup_inputs_huge(rng):
    s = seeds(rng)
    v = rng.random((N, 128, P, 4), dtype=np.float32)
    for r in range(N):
        on = np.isin(np.arange(P), s[r])[None, :, None]
        u = ((0.7 + 0.85 * rng.random(P)) * (1 - 2 * (r % 2)))[None, :, None]
        v[r] = np.where(on, 1.7 + 0.28 * v[r], (0.8 + 0.45 * v[r]) * u)
    return {**plain(rng), "x": big((v * np.float32(2.0 ** 29)).reshape(N, 128, 4 * P)), **lists(rng, graph(rng), s)}
def setup_inputs_spread(rng):
    return {**setup_inputs(rng), "x": big(wide(rng, N, 128, 4 * P, cols=6))}
def setup_inputs_ties(rng):
    g = rng.integers(4, 8, (128, 3, 4)) * np.exp2(rng.integers(-2, 1, (128, 3, 4))) * rng.choice([-1.0, 1.0], (128, 3, 4)) * np.exp2(rng.integers(-2, 3, (128, 3, 1)))
    h = rng.integers(0, 3, (N, P))
    h[::2] = 0
    return {**plain(rng), "x": big(np.stack([g[:, h[r]].reshape(128, -1) for r in range(N)])), **lists(rng, graph(rng), seeds(rng), late=True)}
def check_inputs(d):
    b = []
    for k, low in (("x", 2.0 ** -16), ("w", 2.0 ** -30)):
        v = np.abs(d[k].astype(np.float32))
        if not (np.isfinite(v).all() and ((v == 0) | (v >= low) & (v <= 2.0 ** 30)).all()): b.append("a value of " + k)
    for r in range(N):
        e = entries(d["sd"][r])
        if e.min() < 0 or e.max() >= P or np.unique(e).size != S: b.append("sd")
    e = np.concatenate([entries(d["nb"][r]).reshape(M, P) for r in range(N)], axis=1).astype(np.int64)
    if e.min() < -1 or e.max() >= N * P: return b + ["nb"]
    k, j = np.nonzero(e >= 0)
    n = e[k, j]
    a, c = j * (N * P) + n, n * (N * P) + j
    if (n == j).any() or np.unique(a).size != a.size: b.append("nb names a place twice or itself")
    if not np.array_equal(np.sort(a), np.sort(c)): b.append("nb isn't symmetric")
    for r in range(N):
        for q in range(N):
            if q != r and np.count_nonzero((e[:, P * r:P * r + P] // P == q).any(axis=0)) > B: b.append("places with neighbours on one other rank")
    return b
def reference(x, w, nb, sd):
    first = join(*[mx_ref.quantize(np.ascontiguousarray(x[r])) for r in range(N)])
    now = first
    near = np.concatenate([entries(nb[r]).reshape(M, P) for r in range(N)], axis=1)
    parent = np.full(N * P, -1)
    fresh = np.concatenate([P * r + entries(sd[r]) for r in range(N)])
    parent[fresh] = fresh
    score = np.full((M, N * P), -np.inf, np.float32)
    for t in range(R):
        spot = np.full(N * P + 1, -1)
        spot[fresh] = np.arange(fresh.size)
        side = pick(now, np.concatenate([fresh, np.full(4 + -fresh.size % 4, -1)]))
        z = np.concatenate([mx_ref.matmul(pick(first, np.arange(i, i + 128)), side) for i in range(0, N * P, 128)])
        k, j = np.nonzero(spot[near] >= 0)
        score[k, j] = z[j, spot[near[k, j]]] + np.float32(0)
        best, at = score.max(axis=0), score.argmax(axis=0)
        chosen = []
        for r in range(N):
            mine = np.arange(P * r, P * r + P)
            c = mine[(parent[mine] < 0) & np.isfinite(best[mine])]
            chosen.append(c[np.argsort(-best[c], kind="stable")[:K]])
        fresh = np.concatenate(chosen)
        parent[fresh] = near[at[fresh], fresh]
        pad = np.full(4 + -fresh.size % 4, -1)
        v = decode(pick(now, np.concatenate([fresh, pad, parent[fresh], pad])))
        h = v.shape[1] // 2
        new = mx_ref.quantize(np.ascontiguousarray(((v[:, :h] + v[:, h:]) * np.float32(0.5)).astype(BF)))
        now = put(now, fresh, pick(new, np.arange(fresh.size)))
    y, pa = np.zeros((N, 128, O * P), np.float32), np.zeros((N, 1, P), np.float32)
    oc, osc = np.zeros((N, 128, 4 * P), np.uint8), np.zeros((N, 16, P), np.uint8)
    for r in range(N):
        mine = np.arange(P * r, P * r + P)
        q = pick(now, mine)
        for o in range(O): y[r, :, P * o:P * o + P] = mx_ref.matmul(mx_ref.quantize(np.ascontiguousarray(cut(w[r], o))), q)
        oc[r], osc[r] = emit(q)
        pa[r, 0] = parent[mine]
    return {"y": y, "oc": oc, "osc": osc, "pa": pa}

@@ -1,0 +1,534 @@
+import numpy as np
+from concourse.bass import DstId, RemoteDMATransfer
+from concourse.mybir import dt, AluOpType as Op, AxisListType, ActivationFunctionType as Fn
+
+F8 = "float8_e4m3fn_x4"
+WC = (384, 608, 864)
+WF = 448
+STR, OFF = 304, 48
+TAB, NONE = 2440, 2432
+ZW = 776
+LOW = -9e29
+SCRATCH = {
+    "xt": ("sbuf", [128, 1024], "bfloat16"), "wt": ("sbuf", [128, 1024], "bfloat16"),
+    "qx": ("sbuf", [128, 256], F8), "qxs": ("sbuf", [128, 256], "uint8"),
+    "qw": ("sbuf", [128, 256], F8), "qws": ("sbuf", [128, 256], "uint8"), "half": ("sbuf", [128, 128], "bfloat16"),
+    "et": ("sbuf", [128, 528], "bfloat16"), "eq": ("sbuf", [128, 512], F8), "eqs": ("sbuf", [128, 512], "uint8"),
+    "comb0": ("sbuf", [128, WC[0]], F8), "comb0s": ("sbuf", [128, WC[0]], "uint8"),
+    "comb1": ("sbuf", [128, WC[1]], F8), "comb1s": ("sbuf", [128, WC[1]], "uint8"),
+    "comb2": ("sbuf", [128, WC[2]], F8), "comb2s": ("sbuf", [128, WC[2]], "uint8"),
+    "finw": ("sbuf", [128, WF], F8), "finws": ("sbuf", [128, WF], "uint8"),
+    "fin": ("sbuf", [128, 256], F8), "fins": ("sbuf", [128, 256], "uint8"),
+    "pk": ("sbuf", [128, 128], F8), "pks": ("sbuf", [128, 128], "uint8"),
+    "ht": ("sbuf", [128, 512], "bfloat16"), "od": ("sbuf", [128, 128], "float32"), "own": ("sbuf", [128, 1024], "bfloat16"),
+    "sdw": ("sbuf", [128, 2], "int32"), "nbw": ("sbuf", [128, 64], "int32"), "sdu": ("sbuf", [128, 2], "uint16"),
+    "nbof": ("sbuf", [128, 2], "uint16"), "nboi": ("sbuf", [128, 16], "int32"), "nbsh": ("sbuf", [128, 8], "int32"),
+    "nbo": ("sbuf", [128, 8], "float32"), "nba": ("sbuf", [128, 8], "float32"), "nbn": ("sbuf", [128, 8], "float32"),
+    "nbm": ("sbuf", [128, 8], "float32"), "nb3": ("sbuf", [128, 8], "float32"), "nbu": ("sbuf", [128, 8], "uint16"),
+    "oix": ("sbuf", [128, 2], "uint16"), "olk": ("sbuf", [128, 32], "float32"), "ofl": ("sbuf", [128, 32], "float32"),
+    "pint": ("sbuf", [128, 1], "int32"), "pidx": ("sbuf", [128, 1], "float32"),
+    "c16": ("sbuf", [128, 64], "float32"),
+    "ic": ("sbuf", [128, 256], "float32"), "ci": ("sbuf", [128, 16], "int32"), "cf": ("sbuf", [128, 32], "float32"),
+    "plm": ("sbuf", [128, 256], "float32"), "ste": ("sbuf", [128, 512], "bfloat16"),
+    "ones": ("sbuf", [128, 2], "float32"),
+    "posc": ("sbuf", [128, 768], "float32"), "tab": ("sbuf", [128, TAB], "float32"), "loc": ("sbuf", [128, TAB], "float32"),
+    "hma": ("sbuf", [128, 64], "float32"), "hm": ("sbuf", [128, 128], "float32"),
+    "negm": ("sbuf", [128, 64], "float32"), "segm": ("sbuf", [128, 64], "float32"),
+    "my0": ("sbuf", [128, 2], "uint16"), "my1": ("sbuf", [128, 2], "uint16"), "my2": ("sbuf", [128, 2], "uint16"), "my3": ("sbuf", [128, 2], "uint16"),
+    "land0": ("sbuf", [128, 16], "uint16"), "land1": ("sbuf", [128, 16], "uint16"), "land2": ("sbuf", [128, 16], "uint16"),
+    "lk": ("sbuf", [128, 128], "float32"), "pv": ("sbuf", [128, 128], "float32"), "zo": ("sbuf", [128, 8], "uint16"),
+    "zf": ("sbuf", [128, 8], "float32"),
+    "zsb": ("sbuf", [128, 2 * ZW], "float32"), "gs": ("sbuf", [128, 192], "float32"), "sc": ("sbuf", [128, 192], "float32"),
+    "sbx": ("sbuf", [128, 128], "float32"), "row": ("sbuf", [128, 256], "float32"),
+    "e8": ("sbuf", [128, 8], "float32"), "ne8": ("sbuf", [128, 8], "float32"),
+    "t8": ("sbuf", [128, 8], "float32"), "u8": ("sbuf", [128, 8], "float32"),
+    "sf": ("sbuf", [128, 8], "float32"), "sn": ("sbuf", [128, 8], "float32"), "val": ("sbuf", [128, 2], "float32"),
+    "ed": ("sbuf", [128, 1024], "bfloat16"), "cm": ("sbuf", [128, 1024], "bfloat16"), "sg": ("sbuf", [128, 512], "bfloat16"),
+    "rs": ("sbuf", [128, 2], "float32"), "y2": ("sbuf", [128, 2], "float32"), "z2": ("sbuf", [128, 2], "float32"),
+    "hi": ("sbuf", [128, 2], "int32"), "hf": ("sbuf", [128, 2], "float32"), "pat": ("sbuf", [128, 256], "bfloat16"),
+    "oh": ("sbuf", [128, 512], "bfloat16"), "ohq": ("sbuf", [128, 128], F8), "ohqs": ("sbuf", [128, 128], "uint8"),
+    "dg": ("sbuf", [128, 512], "bfloat16"), "dgq": ("sbuf", [128, 128], F8), "dgqs": ("sbuf", [128, 128], "uint8"),
+    "pl": ("sbuf", [128, 2], "float32"),
+    "offp": ("sbuf", [128, 2], "uint16"), "offo": ("sbuf", [128, 2], "uint16"),
+    "tk0": ("sbuf", [128, 2], "float32"), "tk": ("sbuf", [128, 2], "float32"), "nf": ("sbuf", [128, 2], "float32"),
+    "pa2": ("sbuf", [128, 2], "float32"), "w3": ("sbuf", [128, 2], "float32"),
+    "flx": ("sbuf", [128, 256], "float32"), "fo": ("sbuf", [128, 16], "uint16"), "sy": ("sbuf", [128, 512], "float32"),
+    "dec": ("psum", [128, 2048], "float32"), "zz": ("psum", [128, 2048], "float32"),
+}
+SEMAPHORES = ["v", "s", "p", "gp", "dsd", "dx", "dnb", "dw", "arl0", "arl1", "arl2", "arc0", "arc1", "arc2",
+              "arn0", "arn1", "arn2", "dc0", "dc1", "df0", "df1", "di", "dout", "dpa", "sent"]
+
+
+def r(name, c0, c1, p0=0, p1=128, st=1):
+    return (name, c0, c1, p0, p1, st)
+
+
+def meet(a, b):
+    if a[0] != b[0] or a[1] >= b[2] or b[1] >= a[2] or a[3] >= b[4] or b[3] >= a[4]:
+        return False
+    return not (a[5] == b[5] and a[5] > 1 and (a[1] - b[1]) % a[5])
+
+
+def inside(a, b):
+    return a[1] >= b[1] and a[2] <= b[2] and a[3] >= b[3] and a[4] <= b[4] and b[5] == 1
+
+
+def rank_program(g, core, T, topo):
+    rank = T.rank_of(core)
+    if rank is None:
+        return
+    cores = list(T.cores)
+    n = len(cores)
+    S, P, R = 32, 256, 3
+
+    eng = {"v": g.vector, "s": g.scalar, "p": g.tensor, "y": g.sync, "g": g}
+    own = {"v": "v", "s": "s", "p": "p", "g": "gp"}
+    known = {e: {} for e in eng}
+    cnt = {}
+    hist = {}
+    seq = [0]
+
+    def need(e, toks):
+        for sem, val, clock, q in sorted(toks, key=lambda t: -t[3]):
+            if known[e].get(sem, 0) < val:
+                eng[e].wait_ge(T.sem[sem], val)
+                known[e][sem] = val
+                for k, c in clock.items():
+                    known[e][k] = max(known[e].get(k, 0), c)
+
+    def before(e, reads, writes):
+        toks = []
+        for a in reads:
+            for b, kind, tok, f in hist.get(a[0], []):
+                if kind == "w" and meet(a, b):
+                    toks.append(tok)
+        for a in writes:
+            for b, kind, tok, f in hist.get(a[0], []):
+                if meet(a, b):
+                    toks.append(tok)
+        need(e, toks)
+
+    def note(e, reads, writes, tok):
+        for a in writes:
+            hist[a[0]] = [h for h in hist.get(a[0], []) if not inside(h[0], a)] + [(a, "w", tok, e)]
+        for a in reads:
+            hist[a[0]] = [h for h in hist.get(a[0], []) if not (h[1] == "r" and h[3] == e and inside(h[0], a))] + [(a, "r", tok, e)]
+
+    def token(sem, clock):
+        seq[0] += 1
+        return (sem, cnt[sem], dict(clock), seq[0])
+
+    def op(e, fn, reads, writes):
+        before(e, reads, writes)
+        sem = own[e]
+        cnt[sem] = cnt.get(sem, 0) + 1
+        fn().then_inc(T.sem[sem], 1)
+        note(e, reads, writes, token(sem, known[e]))
+
+    def dmas(sem, lst):
+        for e, out, in_, reads, writes in lst:
+            before(e, reads, writes)
+            cnt[sem] = cnt.get(sem, 0) + 16
+            eng[e].dma_start(out, in_).then_inc(T.sem[sem], 16)
+        for e, out, in_, reads, writes in lst:
+            note(sem, reads, writes, token(sem, {}))
+
+    def ap(q):
+        name, c0, c1, p0, p1, st = q
+        return T[name][p0:p1, c0:c1] if st == 1 else T[name][p0:p1, c0:c1:st]
+
+    def tup(*xs):
+        return [x for x in xs if isinstance(x, tuple)]
+
+    def sv(x):
+        return ap(x) if isinstance(x, tuple) else x
+
+    def ts(out, a, s1, op0, s2=None, op1=None):
+        if op1 is None:
+            op("v", lambda: g.vector.tensor_scalar(ap(out), ap(a), sv(s1), None, op0), [a] + tup(s1), [out])
+        else:
+            op("v", lambda: g.vector.tensor_scalar(ap(out), ap(a), sv(s1), sv(s2), op0, op1), [a] + tup(s1, s2), [out])
+
+    def tt(out, a, b, o):
+        op("v", lambda: g.vector.tensor_tensor(ap(out), ap(a), ap(b), o), [a, b], [out])
+
+    def cp(out, a):
+        op("v", lambda: g.vector.tensor_copy(ap(out), ap(a)), [a], [out])
+
+    def tr(out, a):
+        op("v", lambda: g.vector.transpose(ap(out), ap(a)), [a], [out])
+
+    def scan(out, a, b, init, o0, o1):
+        op("v", lambda: g.vector.tensor_tensor_scan(ap(out), ap(a), ap(b), init, o0, o1), [a, b], [out])
+
+    def fill(out, c):
+        op("v", lambda: g.vector.memset(ap(out), c), [], [out])
+
+    def iota(out, pattern, base, cm, flag=True):
+        if flag:
+            op("g", lambda: g.iota(ap(out), pattern, base, cm, allow_small_or_imprecise_dtypes=True), [], [out])
+        else:
+            op("g", lambda: g.iota(ap(out), pattern, base, cm), [], [out])
+
+    def act(out, a, func, bias=0.0, scale=1.0, accum=None):
+        w = [out] + tup(accum)
+        op("s", lambda: g.scalar.activation(ap(out), ap(a), func, bias=sv(bias), scale=sv(scale), accum_out=None if accum is None else ap(accum)),
+           [a] + tup(bias, scale), w)
+
+    def quant(c, s, a, b, src, x0, x1):
+        op("v", lambda: g.vector.quantize_mx(T[c][:, a:b], T[s][:, a:b], T[src][:, x0:x1]), [r(src, x0, x1)], [r(c, a, b), r(s, a, b)])
+
+    def gather(out, win, off):
+        op("v", lambda: g.vector.tensor_copy(ap(out), ap(win).indirect(ap(off))), [win, off], [out])
+
+    def gather_s(out, win, off):
+        op("s", lambda: g.scalar.activation(ap(out), ap(win).indirect(ap(off)), Fn.Copy), [win, off], [out])
+
+    def scatter(win, off, a):
+        op("v", lambda: g.vector.tensor_copy(ap(win).indirect(ap(off)), ap(a)), [a, off], [win])
+
+    def pick(c2, a2, c1, w, off, o0, o1):
+        k = 16 * (o1 - o0)
+        s2, s1 = c2 + "s", c1 + "s"
+        op("v", lambda: g.vector.tensor_copy(T[c2][:, a2:a2 + k].bitcast(dt.uint32), T[c1][:, 0:w].bitcast(dt.uint32).indirect(T[off][:, o0:o1])),
+           [r(c1, 0, w), r(off, o0, o1)], [r(c2, a2, a2 + k)])
+        op("s", lambda: g.scalar.activation(T[s2][:, a2:a2 + k], T[s1][:, 0:w].indirect(T[off][:, o0:o1]), Fn.Copy),
+           [r(s1, 0, w), r(off, o0, o1)], [r(s2, a2, a2 + k)])
+
+    def mm(out, bank, width, c1, a1, c2, a2):
+        op("p", lambda: g.tensor.matmul_mx(T[out][:, 512 * bank:512 * bank + width], T[c1][:, a1:a1 + 128], T[c1 + "s"][:, a1:a1 + 128],
+                                           T[c2][:, a2:a2 + width], T[c2 + "s"][:, a2:a2 + width], True, True),
+           [r(c1, a1, a1 + 128), r(c1 + "s", a1, a1 + 128), r(c2, a2, a2 + width), r(c2 + "s", a2, a2 + width)],
+           [r(out, 512 * bank, 512 * bank + 512)])
+
+    far = [q for q in range(n) if topo.chip(cores[q]) != topo.chip(core)]
+    near = [q for q in range(n) if q != rank and topo.chip(cores[q]) == topo.chip(core)]
+    mate = rank ^ 1
+    assert near == [mate]
+    fe = topo.engines(core, cores[far[0]])
+    ne = [e for e in topo.engines(core, cores[mate]) if e not in fe][::2]
+    block = lambda q: n - 1 - (q ^ rank)
+
+    def dest(q):
+        a = topo.addr(cores[q])
+        return DstId(rid=a[0], pnc=a[1])
+
+    def send(fsem, nsem, src, dst_of, reads):
+        before("g", reads, [])
+        out = []
+        for qs, es, sem in ((far, fe, fsem), (near, ne, nsem)):
+            out.append(RemoteDMATransfer(dst_ids=[dest(q) for q in qs], dma_engine_mask=sum(1 << e for e in es), remote_sem=T.sem[sem],
+                                         srcs=[src], dsts=[dst_of(q) for q in qs], alu_op=0))
+            cnt["sent"] = cnt.get("sent", 0) + len(es)
+        g.remote_dma_fused(out, local_sem=T.sem["sent"])
+
+    def landed(sem, total, regions):
+        cnt[sem] = total
+        seq[0] += 1
+        for a in regions:
+            note("far", [], [a], (sem, total, {}, seq[0]))
+
+    def send_list(t):
+        send("arl%d" % t, "arl%d" % t, T["my%d" % t][:, 0:2], lambda q: T["land%d" % t][:, 2 * block(q):2 * block(q) + 2], [r("my%d" % t, 0, 2)])
+        landed("arl%d" % t, len(fe) * len(far) + len(ne), [r("land%d" % t, 0, 14)])
+
+    def send_cols(t):
+        c, b, fs, nr = "comb%d" % t, P * t, "arc%d" % t, "arn%d" % t
+        o, w = b + 224, b + 192
+        send(fs, nr, T[c][:, o:o + S].bitcast(dt.uint8), lambda q: T[c][:, b + S * block(q):b + S * block(q) + S].bitcast(dt.uint8), [r(c, o, o + S)])
+        send(fs, nr, T[c + "s"][:, o:o + S], lambda q: T[c + "s"][:, b + S * block(q):b + S * block(q) + S], [r(c + "s", o, o + S)])
+        landed(nr, 2 * len(ne), [r(c, w, w + S), r(c + "s", w, w + S)])
+        landed(fs, 2 * len(fe) * len(far), [r(c, b, w), r(c + "s", b, w)])
+
+    def copies(src, s0, dst, d0, w):
+        return [("y", T[dst][:, d0:d0 + w].bitcast(dt.uint8), T[src][:, s0:s0 + w].bitcast(dt.uint8), [r(src, s0, s0 + w)], [r(dst, d0, d0 + w)]),
+                ("y", T[dst + "s"][:, d0:d0 + w], T[src + "s"][:, s0:s0 + w], [r(src + "s", s0, s0 + w)], [r(dst + "s", d0, d0 + w)])]
+
+    dmas("dsd", [(q, T.sdw[16 * a:16 * a + 16, :], T.sd[:], [], [r("sdw", 0, 2, 16 * a, 16 * a + 16)]) for a, q in enumerate("ys")])
+    dmas("dx", [("y", T.xt[:], T.x[:], [], [r("xt", 0, 1024)])])
+    dmas("dnb", [("y", T.nbw[16 * a:16 * a + 16, :], T.nb[:], [], [r("nbw", 0, 64, 16 * a, 16 * a + 16)]) for a in range(8)])
+    dmas("dw", [("y", T.wt[:], T.w[:], [], [r("wt", 0, 1024)])])
+
+    base = STR * rank + OFF
+    pint, pidx = r("pint", 0, 1), r("pidx", 0, 1)
+    iota(pint, [[0, 1]], 0, 1, False)
+    iota(pidx, [[0, 1]], 0, 1)
+    iota(r("posc", 0, 256), [[1, 256]], 1, 0)
+    ci = lambda i: r("ci", i, i + 1)
+    cf = lambda i: r("cf", i, i + 1)
+    fill(r("ste", 0, 512, st=2), 0.0)
+    fill(r("ste", 1, 512, st=2), 1.0)
+    for b in range(5):
+        act(r("tab", 512 * b, min(512 * b + 512, TAB)), r("ste", 0, min(512, TAB - 512 * b)), Fn.Copy, scale=0.0)
+    fill(r("half", 0, 128), 0.5)
+    fill(r("et", 0, 528), 0.0)
+    e_, h_ = r("et", 3, 515, st=4), r("half", 0, 128)
+    op("g", lambda: g.affine_select(ap(e_), ap(h_), [[-1, 128]], Op.is_equal, 0.0, 0, 1), [h_], [e_])
+    iota(r("c16", 0, 64), [[0, 4], [1, 16]], 0, 0)
+    ts(ci(7), pint, 4, Op.arith_shift_right)
+    ts(ci(0), pint, 31, Op.bitwise_and)
+    ts(ci(1), pint, 15, Op.bitwise_and)
+    ts(ci(2), pint, 96, Op.bitwise_and)
+    ts(ci(3), pint, 32, Op.bitwise_and)
+    ts(ci(4), pint, 64, Op.bitwise_and)
+    ts(ci(5), pint, 3, Op.bitwise_and)
+    ts(ci(6), pint, 4, Op.bitwise_and)
+    cp(cf(10), pidx)
+    cp(r("cf", 0, 8), r("ci", 0, 8))
+    ts(cf(11), pidx, 128.0, Op.add)
+    ts(cf(17), cf(5), -16.0, Op.mult, cf(7), Op.add)
+
+    for b in range(4):
+        ts(r("my0", 0, 2, 32 * b, 32 * b + 32), r("sdw", 0, 2, 0, 32), float(base), Op.add)
+    send_list(0)
+    for b in range(4):
+        cp(r("sdu", 0, 2, 32 * b, 32 * b + 32), r("sdw", 0, 2, 0, 32))
+    place2 = r("cf", 10, 12)
+    quant("qx", "qxs", 0, 256, "xt", 0, 1024)
+    pick("comb0", 224, "qx", 256, "sdu", 0, 2)
+    send_cols(0)
+    dmas("di", copies("qx", 0, "comb0", 256, 128) + copies("qx", 32, "pk", 32, 96))
+
+    iota(r("ic", 0, 256), [[32, 4], [128, 2], [1, 32]], 0, 0)
+    iota(r("dg", 0, 512), [[0, 512]], 0, 0)
+    iota(r("pat", 0, 256), [[0, 8], [-2, 16], [-32, 2]], 256, 0)
+    iota(r("posc", 256, 768), [[1, 512]], 257, 0)
+    iota(r("loc", base, base + P), [[1, P]], 0, 0)
+    iota(r("ht", 0, 512), [[0, 512]], 0, 0)
+
+    tab = r("tab", 0, TAB)
+    for b in range(4):
+        quant("eq", "eqs", 128 * b, 128 * b + 128, "et", 3 - b, 515 - b)
+    ts(cf(18), cf(6), 2.0, Op.mult, 48.0, Op.add)
+    ts(cf(19), cf(1), -1024.0, Op.mult, 15360.0, Op.add)
+    ts(cf(25), cf(1), 16.0, Op.add)
+    tt(r("nbof", 0, 1), cf(17), cf(18), Op.add)
+    ts(r("oix", 0, 2), place2, float(base), Op.add)
+    ts(r("hma", 0, 64), r("c16", 0, 64), cf(1), Op.is_equal)
+    for b in range(2):
+        act(r("hm", 64 * b, 64 * b + 64), r("hma", 0, 64), Fn.Copy, bias=1024.0, scale=-66560.0)
+    for b in range(4):
+        mm("dec", b, 256, "eq", 128 * b, "qx", 0)
+        act(r("own", 256 * b, 256 * b + 256), r("dec", 512 * b, 512 * b + 256), Fn.Copy)
+    op("v", lambda: g.vector.tensor_copy(T.nboi[:, 0:16], T.nbw[:, 0:64].indirect(T.nbof[:, 0:1])), [r("nbw", 0, 64), r("nbof", 0, 1)], [r("nboi", 0, 16)])
+    scatter(tab, r("my0", 0, 2), r("posc", 224, 256))
+    nbi, nbo, nb3 = r("nboi", 0, 8), r("nbo", 0, 8), r("nb3", 0, 8)
+    ts(r("nbsh", 0, 8), nbi, 8, Op.arith_shift_right)
+    cp(nbo, nbi)
+    gather(r("olk", 0, 32), tab, r("oix", 0, 2))
+    ts(r("nba", 0, 8), r("nbsh", 0, 8), float(STR - P), Op.mult, float(OFF - NONE), Op.add)
+    ts(r("nbn", 0, 8), nbo, 0.0, Op.is_lt, float(NONE + 1 + STR - P - OFF), Op.mult)
+
+    def run_on(out, a, width):
+        scan(out, r("hm", 0, width), a, 0.0, Op.add, Op.max)
+
+    run_on(r("ofl", 0, 32), r("olk", 0, 32), 32)
+    tt(r("nba", 0, 8), r("nba", 0, 8), nbo, Op.add)
+    ts(cf(21), cf(3), -2.0, Op.mult, cf(2), Op.add)
+    ts(r("tk0", 0, 2), r("ofl", 15, 32, st=16), cf(19), Op.subtract, 0.0, Op.is_gt)
+    tt(r("nbm", 0, 8), r("nba", 0, 8), r("nbn", 0, 8), Op.add)
+    ts(cf(22), cf(4), -2.0, Op.mult, cf(2), Op.add)
+    ts(cf(23), cf(4), -2.0, Op.mult, cf(21), Op.add)
+
+    def settle(first):
+        if first:
+            ts(r("nf", 0, 2), r("tk0", 0, 2), -1.0, Op.mult, 1.0, Op.add)
+            ts(r("cf", 12, 14), place2, -0.5, Op.add, -2.0 ** -120, Op.mult)
+        else:
+            tt(r("nf", 0, 2), r("nf", 0, 2), r("tk", 0, 2), Op.subtract)
+        for h in (0, 1):
+            ts(r("nbu", 4 * h, 4 * h + 4), r("nbm", 4 * h, 4 * h + 4), r("nf", h, h + 1), Op.mult, float(NONE), Op.add)
+
+    def masks(t):
+        scatter(tab, r("land%d" % t, 0, 14), r("posc", P * t, P * t + 224))
+        gather(r("lk", 0, 128), tab, r("nbu", 0, 8))
+        run_on(r("pv", 0, 128), r("lk", 0, 128), 128)
+        ts(r("zo", 0, 8), r("pv", 15, 128, st=16), cf(19), Op.subtract)
+        ts(r("zf", 0, 8), r("pv", 15, 128, st=16), cf(19), Op.subtract, -1.0, Op.add)
+
+    settle(True)
+    for d, b in enumerate((2, 21, 22, 23)):
+        act(r("plm", 64 * d, 64 * d + 64), r("ic", 64 * d, 64 * d + 64), Fn.Identity, bias=cf(b))
+    for h in (0, 1):
+        act(r("ed", 512 * h + 1, 512 * h + 512, st=2), r("plm", 0, 256), Fn.Identity, bias=r("cf", 12 + h, 13 + h), scale=2.0 ** -120)
+    masks(0)
+    fill(r("ones", 0, 2), 1.0)
+    for h in (0, 1):
+        fill(r("zsb", ZW * h, ZW * h + 1), LOW)
+        fill(r("gs", 96 * h + 64, 96 * h + 96), LOW)
+    ts(r("negm", 0, 64), r("c16", 0, 64), cf(1), Op.not_equal, LOW, Op.mult)
+    ts(r("segm", 0, 64), r("c16", 0, 64), 0.0, Op.is_equal, LOW, Op.mult)
+
+    def digits(h):
+        ts(r("dg", 16 + h, 23 + h, st=6), r("ones", 0, 2), cf(2), Op.mult, float(OFF + 16 + 128 * h), Op.add)
+        ts(r("dg", 48 + 6 * h, 50 + 6 * h), r("ones", 0, 2), cf(0), Op.mult, -16.0, Op.add)
+
+    digits(0)
+
+    def move(e, out, a):
+        if e == "v":
+            cp(out, a)
+        else:
+            act(out, a, Fn.Copy)
+
+    for t in range(R):
+        c = "comb%d" % t
+        more = t < R - 1
+        zs = lambda h, a, w: r("zsb", ZW * h + 1 + P * t + a, ZW * h + 1 + P * t + a + w)
+        for h in (0, 1):
+            mm("zz", 2 + h, 128, "qx", 128 * h, c, P * t + 192)
+            act(zs(h, 192, 64), r("zz", 1024 + 512 * h, 1088 + 512 * h), Fn.Copy)
+        for h in (0, 1):
+            mm("zz", h, 192, "qx", 128 * h, c, P * t)
+            act(zs(h, 0, 192), r("zz", 512 * h, 512 * h + 192), Fn.Copy)
+
+        def scores(h):
+            w, o, q = r("zsb", ZW * h, ZW * h + 1 + P * t + P), r("zo", 4 * h, 4 * h + 4), r("gs", 96 * h, 96 * h + 64)
+            op("v", lambda: g.vector.tensor_tensor(ap(q), ap(w).indirect(ap(o)), T.negm[:, 0:64], Op.add), [w, o, r("negm", 0, 64)], [q])
+
+        def own_scores(h):
+            scan(r("sbx", 64 * h, 64 * h + 64), r("segm", 0, 64), r("gs", 96 * h, 96 * h + 64), LOW, Op.add, Op.max)
+
+        sb = lambda h: r("sbx", 15 + 64 * h, 64 + 64 * h, st=16)
+        bst = lambda h: r("sc", 96 * h + 95, 96 * h + 96)
+        k4 = lambda name, h: r(name, 4 * h, 4 * h + 4)
+        isbest = lambda h: ts(k4("e8", h), sb(h), bst(h), Op.is_equal)
+        scores(0)
+        if t == 0:
+            digits(1)
+        scores(1)
+        for h in (0, 1):
+            a = r("gs", 96 * h, 96 * h + 96)
+            scan(r("sc", 96 * h, 96 * h + 96), a, a, LOW, Op.max, Op.max)
+        for h in (0, 1):
+            tr(r("row", 32 * h, 32 * h + 32), r("sc", 96 * h + 64, 96 * h + 96))
+        if more:
+            lst = []
+            for t2 in range(t + 1, R):
+                lst += copies(c, P * t, "comb%d" % t2, P * t, P)
+            if t == 0:
+                lst += copies("qx", 0, "finw", 0, P)
+            dmas("dc%d" % t, lst)
+        own_scores(0)
+        for b in range(4):
+            move("v" if b < 2 else "s", r("row", 64, 128, 32 * b, 32 * b + 32), r("row", 0, 64, 32 * (b ^ 1), 32 * (b ^ 1) + 32))
+        own_scores(1)
+        for b in (0, 1):
+            move("v" if b < 1 else "s", r("row", 128, 256, 64 * b, 64 * b + 64), r("row", 0, 128, 64 * (1 - b), 64 * (1 - b) + 64))
+        isbest(0)
+        isbest(1)
+
+        def differ(e, h, i):
+            a, o = r("row", 128 * i, 128 * i + 128), r("ed", 512 * h + 256 * i, 512 * h + 256 * i + 256, st=2)
+            if e == "v":
+                ts(o, a, -1.0, Op.mult, bst(h), Op.add)
+            else:
+                act(o, a, Fn.Identity, bias=bst(h), scale=-1.0)
+
+        differ("v", 0, 0)
+        tt(r("t8", 0, 8), r("e8", 0, 8), r("zf", 0, 8), Op.mult)
+        differ("s", 0, 1)
+        differ("s", 1, 0)
+        differ("s", 1, 1)
+        for h in (0, 1):
+            act(k4("ne8", h), sb(h), Fn.Sign, bias=bst(h), scale=-1.0)
+
+        def ahead(x, w):
+            scan(r("cm", x, x + w), r("ste", 0, w), r("ed", x, x + w), 0.0, Op.mult, Op.add)
+
+        def count(h):
+            act(r("sg", 256 * h, 256 * h + 256), r("cm", 512 * h + 1, 512 * h + 512, st=2), Fn.Sign, accum=r("rs", h, h + 1))
+
+        ahead(0, 256)
+        ahead(256, 256)
+        count(0)
+        ahead(512, 512)
+        count(1)
+        scan(r("sf", 0, 8), r("ne8", 0, 8), r("t8", 0, 8), 0.0, Op.mult, Op.add)
+        ts(r("val", 0, 2), r("sc", 95, 192, st=96), -1e29, Op.is_gt)
+        loc2 = r("sf", 3, 8, st=4)
+        top = 8 if t == 2 else 0
+        ts(r("hi", 0, 2), loc2, 1.0 / 32, Op.mult)
+
+        def slots(h):
+            ts(r("oh", h, 512, st=2), r("pat", 0, 256), r("rs", h, h + 1), Op.is_equal, r("val", h, h + 1), Op.mult)
+
+        slots(0)
+        ts(r("hf", 0, 2), r("hi", 0, 2), 32.0, Op.mult)
+        for u in (0, 1):
+            act(r("dg", 6 * u, 6 * u + 2), r("hf", 0, 2), Fn.Copy, bias=-32.0 * top)
+            tt(r("dg", 32 + 6 * u, 34 + 6 * u), loc2, r("hf", 0, 2), Op.subtract)
+        slots(1)
+        quant("dgq", "dgqs", 0, 128, "dg", 0, 512)
+        quant("ohq", "ohqs", 0, 128, "oh", 0, 512)
+        mm("zz", 2, 128, "ohq", 0, "dgq", 0)
+        if t == 0:
+            ts(nb3, nbo, 1.0, Op.add)
+        ts(r("tk", 0, 1), r("rs", 0, 1), 193.0, Op.is_gt, r("val", 0, 1), Op.mult)
+        ts(r("tk", 1, 2), r("rs", 1, 2), 193.0, Op.is_gt, r("val", 1, 2), Op.mult)
+        tt(r("u8", 0, 8), r("e8", 0, 8), nb3, Op.mult)
+        scan(r("sn", 0, 8), r("ne8", 0, 8), r("u8", 0, 8), 0.0, Op.mult, Op.add)
+        out = lambda i: r("zz", 1024 + i, 1025 + i)
+        for u in (0, 1):
+            ts(r("offp", u, u + 1), out(u), out(8 + u), Op.add, 32.0 * top, Op.add)
+        for u, k in enumerate((1, 25)):
+            ts(r("pl", u, u + 1), out(4 + u), out(12 + u), Op.add, cf(k), Op.max)
+        pick("pk", 0, c, P * t + P, "offp", 0, 2)
+        ts(r("offo", 0, 2), r("pl", 0, 2), -float(OFF), Op.add, 0.0, Op.max)
+        for b in range(4):
+            gather_s(r("od", 32 * b, 32 * b + 32), r("own", 256 * b, 256 * b + 256), r("offo", 0, 2))
+        my = "my%d" % (t + 1)
+        ts(r(my, 0, 2), r("pl", 0, 2), float(STR * rank), Op.add)
+        if more:
+            send_list(t + 1)
+
+        def parents():
+            if t == 0:
+                ts(r("z2", 0, 2), place2, float(P * rank + 1), Op.add)
+                tt(r("w3", 0, 2), r("z2", 0, 2), r("tk0", 0, 2), Op.mult)
+                ts(r("pa2", 0, 2), r("w3", 0, 2), -1.0, Op.add)
+            tt(r("y2", 0, 2), r("sn", 3, 8, st=4), r("tk", 0, 2), Op.mult)
+            tt(r("pa2", 0, 2), r("pa2", 0, 2), r("y2", 0, 2), Op.add)
+
+        for b in range(4):
+            mm("dec", b, 128, "eq", 128 * b, "pk", 0)
+        lv = P - 1 + S * t
+        scatter(r("loc", 0, TAB), r(my, 0, 2), r("posc", lv, lv + S))
+        if not more:
+            parents()
+            dmas("dpa", [("y", T.pa[0:1, 128 * h:128 * h + 128], T.pa2[:, h:h + 1], [r("pa2", h, h + 1)], []) for h in (0, 1)])
+        half_row = lambda m: run_on(r("flx", 128 * m, 128 * m + 128), r("loc", base + 128 * m, base + 128 * m + 128), 128)
+        half_list = lambda m: ts(r("fo", 8 * m, 8 * m + 8), r("flx", 128 * m + 15, 128 * m + 128, st=16), cf(19), Op.subtract)
+        for b in range(4):
+            tt(r("ht", b, 128, st=4), r("dec", 512 * b, 512 * b + 32), r("od", 32 * b, 32 * b + 32), Op.add)
+            if not more and b < 2:
+                half_row(b)
+            elif not more:
+                half_list(b - 2)
+        if more:
+            d, o = "comb%d" % (t + 1), P * (t + 1) + 224
+            quant(d, d + "s", o, o + 128, "ht", 0, 512)
+            send_cols(t + 1)
+            dmas("df%d" % t, copies(d, o, "finw", P + S * t, S))
+            scatter(tab, r(my, 0, 2), r("posc", P * (t + 1) + 224, P * (t + 1) + 256))
+            settle(False)
+            masks(t + 1)
+            parents()
+            if t == 0:
+                quant("qw", "qws", 0, 256, "wt", 0, 1024)
+        else:
+            quant("finw", "finws", 320, 448, "ht", 0, 512)
+
+    for m in (0, 1):
+        pick("fin", 128 * m, "finw", 352, "fo", 8 * m, 8 * m + 8)
+        for o in (0, 1):
+            mm("zz", 2 * m + o, 128, "qw", 128 * o, "fin", 128 * m)
+    for m in (0, 1):
+        cp(r("sy", 128 * m, 128 * m + 128), r("zz", 1024 * m, 1024 * m + 128))
+        act(r("sy", 256 + 128 * m, 384 + 128 * m), r("zz", 1024 * m + 512, 1024 * m + 640), Fn.Copy)
+    dmas("dout", [("y", T.oc[:], T.fin[:].bitcast(dt.uint8), [r("fin", 0, 256)], [])] +
+         [("y", T.osc[4 * k:4 * k + 4, :], T.fins[32 * k:32 * k + 4, :], [r("fins", 0, 256)], []) for k in range(4)] +
+         [(q, T.y[:, 256 * o:256 * o + 256], T.sy[:, 256 * o:256 * o + 256], [r("sy", 256 * o, 256 * o + 256)], []) for o, q in enumerate("ys")])
+    for sem in cnt:
+        if known["g"].get(sem, 0) < cnt[sem]:
+            g.wait_ge(T.sem[sem], cnt[sem])

@@ -3,60 +3,33 @@ from concourse.bass import DstId, RemoteDMATransfer
 from concourse.mybir import dt, AluOpType as Op, AxisListType, ActivationFunctionType as Fn
 
 F8 = "float8_e4m3fn_x4"
-WC = (384, 608, 864)
-WF = 448
+WC, WF = 384, 448
 STR, OFF = 304, 48
 TAB, NONE = 2440, 2432
 ZW = 776
+PW = 768
+STEP32 = 1.5 * 2.0 ** 28
 LOW = -9e29
-SCRATCH = {
-    "xt": ("sbuf", [128, 1024], "bfloat16"), "wt": ("sbuf", [128, 1024], "bfloat16"),
-    "qx": ("sbuf", [128, 256], F8), "qxs": ("sbuf", [128, 256], "uint8"),
-    "qw": ("sbuf", [128, 256], F8), "qws": ("sbuf", [128, 256], "uint8"), "half": ("sbuf", [128, 128], "bfloat16"),
-    "et": ("sbuf", [128, 528], "bfloat16"), "eq": ("sbuf", [128, 512], F8), "eqs": ("sbuf", [128, 512], "uint8"),
-    "comb0": ("sbuf", [128, WC[0]], F8), "comb0s": ("sbuf", [128, WC[0]], "uint8"),
-    "comb1": ("sbuf", [128, WC[1]], F8), "comb1s": ("sbuf", [128, WC[1]], "uint8"),
-    "comb2": ("sbuf", [128, WC[2]], F8), "comb2s": ("sbuf", [128, WC[2]], "uint8"),
-    "finw": ("sbuf", [128, WF], F8), "finws": ("sbuf", [128, WF], "uint8"),
-    "fin": ("sbuf", [128, 256], F8), "fins": ("sbuf", [128, 256], "uint8"),
-    "pk": ("sbuf", [128, 128], F8), "pks": ("sbuf", [128, 128], "uint8"),
-    "ht": ("sbuf", [128, 512], "bfloat16"), "od": ("sbuf", [128, 128], "float32"), "own": ("sbuf", [128, 1024], "bfloat16"),
-    "sdw": ("sbuf", [128, 2], "int32"), "nbw": ("sbuf", [128, 64], "int32"), "sdu": ("sbuf", [128, 2], "uint16"),
-    "nbof": ("sbuf", [128, 2], "uint16"), "nboi": ("sbuf", [128, 16], "int32"), "nbsh": ("sbuf", [128, 8], "int32"),
-    "nbo": ("sbuf", [128, 8], "float32"), "nba": ("sbuf", [128, 8], "float32"), "nbn": ("sbuf", [128, 8], "float32"),
-    "nbm": ("sbuf", [128, 8], "float32"), "nb3": ("sbuf", [128, 8], "float32"), "nbu": ("sbuf", [128, 8], "uint16"),
-    "oix": ("sbuf", [128, 2], "uint16"), "olk": ("sbuf", [128, 32], "float32"), "ofl": ("sbuf", [128, 32], "float32"),
-    "pint": ("sbuf", [128, 1], "int32"), "pidx": ("sbuf", [128, 1], "float32"),
-    "c16": ("sbuf", [128, 64], "float32"),
-    "ic": ("sbuf", [128, 256], "float32"), "ci": ("sbuf", [128, 16], "int32"), "cf": ("sbuf", [128, 32], "float32"),
-    "plm": ("sbuf", [128, 256], "float32"), "ste": ("sbuf", [128, 512], "bfloat16"),
-    "ones": ("sbuf", [128, 2], "float32"),
-    "posc": ("sbuf", [128, 768], "float32"), "tab": ("sbuf", [128, TAB], "float32"), "loc": ("sbuf", [128, TAB], "float32"),
-    "hma": ("sbuf", [128, 64], "float32"), "hm": ("sbuf", [128, 128], "float32"),
-    "negm": ("sbuf", [128, 64], "float32"), "segm": ("sbuf", [128, 64], "float32"),
-    "my0": ("sbuf", [128, 2], "uint16"), "my1": ("sbuf", [128, 2], "uint16"), "my2": ("sbuf", [128, 2], "uint16"), "my3": ("sbuf", [128, 2], "uint16"),
-    "land0": ("sbuf", [128, 16], "uint16"), "land1": ("sbuf", [128, 16], "uint16"), "land2": ("sbuf", [128, 16], "uint16"),
-    "lk": ("sbuf", [128, 128], "float32"), "pv": ("sbuf", [128, 128], "float32"), "zo": ("sbuf", [128, 8], "uint16"),
-    "zf": ("sbuf", [128, 8], "float32"),
-    "zsb": ("sbuf", [128, 2 * ZW], "float32"), "gs": ("sbuf", [128, 192], "float32"), "sc": ("sbuf", [128, 192], "float32"),
-    "sbx": ("sbuf", [128, 128], "float32"), "row": ("sbuf", [128, 256], "float32"),
-    "e8": ("sbuf", [128, 8], "float32"), "ne8": ("sbuf", [128, 8], "float32"),
-    "t8": ("sbuf", [128, 8], "float32"), "u8": ("sbuf", [128, 8], "float32"),
-    "sf": ("sbuf", [128, 8], "float32"), "sn": ("sbuf", [128, 8], "float32"), "val": ("sbuf", [128, 2], "float32"),
-    "ed": ("sbuf", [128, 1024], "bfloat16"), "cm": ("sbuf", [128, 1024], "bfloat16"), "sg": ("sbuf", [128, 512], "bfloat16"),
-    "rs": ("sbuf", [128, 2], "float32"), "y2": ("sbuf", [128, 2], "float32"), "z2": ("sbuf", [128, 2], "float32"),
-    "hi": ("sbuf", [128, 2], "int32"), "hf": ("sbuf", [128, 2], "float32"), "pat": ("sbuf", [128, 256], "bfloat16"),
-    "oh": ("sbuf", [128, 512], "bfloat16"), "ohq": ("sbuf", [128, 128], F8), "ohqs": ("sbuf", [128, 128], "uint8"),
-    "dg": ("sbuf", [128, 512], "bfloat16"), "dgq": ("sbuf", [128, 128], F8), "dgqs": ("sbuf", [128, 128], "uint8"),
-    "pl": ("sbuf", [128, 2], "float32"),
-    "offp": ("sbuf", [128, 2], "uint16"), "offo": ("sbuf", [128, 2], "uint16"),
-    "tk0": ("sbuf", [128, 2], "float32"), "tk": ("sbuf", [128, 2], "float32"), "nf": ("sbuf", [128, 2], "float32"),
-    "pa2": ("sbuf", [128, 2], "float32"), "w3": ("sbuf", [128, 2], "float32"),
-    "flx": ("sbuf", [128, 256], "float32"), "fo": ("sbuf", [128, 16], "uint16"), "sy": ("sbuf", [128, 512], "float32"),
-    "dec": ("psum", [128, 2048], "float32"), "zz": ("psum", [128, 2048], "float32"),
-}
-SEMAPHORES = ["v", "s", "p", "gp", "dsd", "dx", "dnb", "dw", "arl0", "arl1", "arl2", "arc0", "arc1", "arc2",
-              "arn0", "arn1", "arn2", "dc0", "dc1", "df0", "df1", "di", "dout", "dpa", "sent"]
+SCRATCH = {"dec": ("psum", [128, 2048], "float32"), "zz": ("psum", [128, 2048], "float32")}
+for _n, _w in (("qx", 256), ("qw", 256), ("eq", 512), ("comb0", WC), ("comb1", WC), ("comb2", WC), ("finw", WF), ("fin", 256),
+               ("ohq", 128), ("dgq", 128), ("dpq", 128)):
+    SCRATCH[_n] = ("sbuf", [128, _w], F8)
+    SCRATCH[_n + "s"] = ("sbuf", [128, _w], "uint8")
+for _d, _l in (("bfloat16", (("xt", 1024), ("wt", 1024), ("half", 128), ("et", 528), ("par", 4 * PW), ("ht", 512), ("own", 4 * STR), ("ste", 512),
+                             ("ed", 1024), ("cm", 1024), ("sg", 512), ("pat", 256), ("oh", 512), ("dg", 512))),
+               ("int32", (("sdw", 2), ("nbw", 64), ("nboi", 16), ("nbsh", 8), ("pint", 1), ("ci", 16))),
+               ("uint16", (("sdu", 2), ("nbof", 2), ("nbu", 8), ("oix", 2), ("my0", 2), ("my1", 2), ("my2", 2), ("land0", 16), ("land1", 16),
+                           ("land2", 16), ("lnr0", 2), ("lnr1", 2), ("lnr2", 2), ("zo", 8), ("pl", 2), ("offp", 2), ("fo", 16))),
+               ("float32", (("yb", 64), ("od", 128), ("nbo", 8), ("nba", 8), ("nbn", 8), ("nbm", 8), ("nb3", 8), ("olk", 32), ("ofl", 32),
+                            ("pidx", 1), ("c16", 64), ("ic", 256), ("cf", 32), ("plm", 256), ("ones", 2), ("posc", 768), ("tab", TAB),
+                            ("loc", TAB), ("hma", 64), ("hm", 128), ("negm", 64), ("segm", 64), ("lk", 128), ("pv", 128), ("zf", 8),
+                            ("zsb", 2 * ZW), ("gs", 192), ("sc", 192), ("sbx", 128), ("row", 256), ("e8", 8), ("ne8", 8), ("t8", 8),
+                            ("u8", 8), ("sf", 8), ("sn", 8), ("val", 2), ("rs", 2), ("y2", 2), ("z2", 2), ("hf", 2), ("tk0", 2),
+                            ("tk", 2), ("nf", 2), ("pa2", 2), ("w3", 2), ("flx", 256), ("sy", 2 * STR)))):
+    for _n, _w in _l:
+        SCRATCH[_n] = ("sbuf", [128, _w], _d)
+SEMAPHORES = ["v", "s", "p", "gp", "dsd", "dx", "dnb", "dw", "arl0", "arl1", "arl2", "arm0", "arm1", "arm2", "arc0", "arc1", "arc2",
+              "ard0", "ard1", "ard2", "arn0", "arn1", "arn2", "dc0", "df0", "df1", "di", "dout", "dpa", "sent"]
 
 
 def r(name, c0, c1, p0=0, p1=128, st=1):
@@ -208,15 +181,18 @@ def rank_program(g, core, T, topo):
     fe = topo.engines(core, cores[far[0]])
     ne = [e for e in topo.engines(core, cores[mate]) if e not in fe][::2]
     block = lambda q: n - 1 - (q ^ rank)
+    far.sort(key=block)
 
     def dest(q):
         a = topo.addr(cores[q])
         return DstId(rid=a[0], pnc=a[1])
 
-    def send(fsem, nsem, src, dst_of, reads):
+    def send(fsem, nsem, src, dst_of, reads, fars=far, nears=near):
         before("g", reads, [])
         out = []
-        for qs, es, sem in ((far, fe, fsem), (near, ne, nsem)):
+        for qs, es, sem in ((fars, fe, fsem), (nears, ne, nsem)):
+            if not qs:
+                continue
             out.append(RemoteDMATransfer(dst_ids=[dest(q) for q in qs], dma_engine_mask=sum(1 << e for e in es), remote_sem=T.sem[sem],
                                          srcs=[src], dsts=[dst_of(q) for q in qs], alu_op=0))
             cnt["sent"] = cnt.get("sent", 0) + len(es)
@@ -229,22 +205,27 @@ def rank_program(g, core, T, topo):
             note("far", [], [a], (sem, total, {}, seq[0]))
 
     def send_list(t):
-        send("arl%d" % t, "arl%d" % t, T["my%d" % t][:, 0:2], lambda q: T["land%d" % t][:, 2 * block(q):2 * block(q) + 2], [r("my%d" % t, 0, 2)])
-        landed("arl%d" % t, len(fe) * len(far) + len(ne), [r("land%d" % t, 0, 14)])
+        to = lambda q: T["lnr%d" % t][:, 0:2] if q == mate else T["land%d" % t][:, 2 * block(q):2 * block(q) + 2]
+        send("arl%d" % t, "arm%d" % t, T["my%d" % t][:, 0:2], to, [r("my%d" % t, 0, 2)])
+        landed("arm%d" % t, len(ne), [r("lnr%d" % t, 0, 2)])
+        landed("arl%d" % t, len(fe) * len(far), [r("land%d" % t, 0, 12)])
 
     def send_cols(t):
-        c, b, fs, nr = "comb%d" % t, P * t, "arc%d" % t, "arn%d" % t
-        o, w = b + 224, b + 192
-        send(fs, nr, T[c][:, o:o + S].bitcast(dt.uint8), lambda q: T[c][:, b + S * block(q):b + S * block(q) + S].bitcast(dt.uint8), [r(c, o, o + S)])
-        send(fs, nr, T[c + "s"][:, o:o + S], lambda q: T[c + "s"][:, b + S * block(q):b + S * block(q) + S], [r(c + "s", o, o + S)])
+        c, fs, nr = "comb%d" % t, "arc%d" % t, "arn%d" % t
+        o, w = 224, 192
+        send(fs, nr, T[c][:, o:o + S].bitcast(dt.uint8), lambda q: T[c][:, S * block(q):S * block(q) + S].bitcast(dt.uint8), [r(c, o, o + S)])
+        to = lambda q: T[c + "s"][:, S * block(q):S * block(q) + S]
+        send(fs, nr, T[c + "s"][:, o:o + S], to, [r(c + "s", o, o + S)], far[:4])
+        send("ard%d" % t, nr, T[c + "s"][:, o:o + S], to, [r(c + "s", o, o + S)], far[4:], [])
         landed(nr, 2 * len(ne), [r(c, w, w + S), r(c + "s", w, w + S)])
-        landed(fs, 2 * len(fe) * len(far), [r(c, b, w), r(c + "s", b, w)])
+        landed(fs, len(fe) * (len(far) + 4), [r(c, 0, w), r(c + "s", 0, 4 * S)])
+        landed("ard%d" % t, len(fe) * (len(far) - 4), [r(c + "s", 4 * S, w)])
 
     def copies(src, s0, dst, d0, w):
         return [("y", T[dst][:, d0:d0 + w].bitcast(dt.uint8), T[src][:, s0:s0 + w].bitcast(dt.uint8), [r(src, s0, s0 + w)], [r(dst, d0, d0 + w)]),
                 ("y", T[dst + "s"][:, d0:d0 + w], T[src + "s"][:, s0:s0 + w], [r(src + "s", s0, s0 + w)], [r(dst + "s", d0, d0 + w)])]
 
-    dmas("dsd", [(q, T.sdw[16 * a:16 * a + 16, :], T.sd[:], [], [r("sdw", 0, 2, 16 * a, 16 * a + 16)]) for a, q in enumerate("ys")])
+    dmas("dsd", [(q, T.sdw[16 * a:16 * a + 16, :], T.sd[:], [], [r("sdw", 0, 2, 16 * a, 16 * a + 16)]) for a, q in enumerate("ysys")])
     dmas("dx", [("y", T.xt[:], T.x[:], [], [r("xt", 0, 1024)])])
     dmas("dnb", [("y", T.nbw[16 * a:16 * a + 16, :], T.nb[:], [], [r("nbw", 0, 64, 16 * a, 16 * a + 16)]) for a in range(8)])
     dmas("dw", [("y", T.wt[:], T.w[:], [], [r("wt", 0, 1024)])])
@@ -258,13 +239,16 @@ def rank_program(g, core, T, topo):
     cf = lambda i: r("cf", i, i + 1)
     fill(r("ste", 0, 512, st=2), 0.0)
     fill(r("ste", 1, 512, st=2), 1.0)
-    for b in range(5):
-        act(r("tab", 512 * b, min(512 * b + 512, TAB)), r("ste", 0, min(512, TAB - 512 * b)), Fn.Copy, scale=0.0)
+
+    def zeros(name, a, w):
+        act(r(name, a, a + w), r("ste", 0, w), Fn.Copy, scale=0.0)
+
+    for b in range(3):
+        zeros("tab", 512 * b, 512)
     fill(r("half", 0, 128), 0.5)
     fill(r("et", 0, 528), 0.0)
     e_, h_ = r("et", 3, 515, st=4), r("half", 0, 128)
     op("g", lambda: g.affine_select(ap(e_), ap(h_), [[-1, 128]], Op.is_equal, 0.0, 0, 1), [h_], [e_])
-    iota(r("c16", 0, 64), [[0, 4], [1, 16]], 0, 0)
     ts(ci(7), pint, 4, Op.arith_shift_right)
     ts(ci(0), pint, 31, Op.bitwise_and)
     ts(ci(1), pint, 15, Op.bitwise_and)
@@ -275,26 +259,30 @@ def rank_program(g, core, T, topo):
     ts(ci(6), pint, 4, Op.bitwise_and)
     cp(cf(10), pidx)
     cp(r("cf", 0, 8), r("ci", 0, 8))
+
+    for b in range(2):
+        ts(r("my0", 0, 2, 64 * b, 64 * b + 64), r("sdw", 0, 2, 0, 64), float(base), Op.add)
+    send_list(0)
+    iota(r("c16", 0, 64), [[0, 4], [1, 16]], 0, 0)
+    for b in range(2):
+        cp(r("sdu", 0, 2, 64 * b, 64 * b + 64), r("sdw", 0, 2, 0, 64))
     ts(cf(11), pidx, 128.0, Op.add)
     ts(cf(17), cf(5), -16.0, Op.mult, cf(7), Op.add)
-
-    for b in range(4):
-        ts(r("my0", 0, 2, 32 * b, 32 * b + 32), r("sdw", 0, 2, 0, 32), float(base), Op.add)
-    send_list(0)
-    for b in range(4):
-        cp(r("sdu", 0, 2, 32 * b, 32 * b + 32), r("sdw", 0, 2, 0, 32))
+    fill(r("dg", 0, 512), 0.0)
     place2 = r("cf", 10, 12)
     quant("qx", "qxs", 0, 256, "xt", 0, 1024)
     pick("comb0", 224, "qx", 256, "sdu", 0, 2)
     send_cols(0)
-    dmas("di", copies("qx", 0, "comb0", 256, 128) + copies("qx", 32, "pk", 32, 96))
+    dmas("di", copies("qx", 0, "comb0", 256, 128))
+    dmas("dc0", copies("qx", 0, "finw", 0, P))
+    zeros("tab", 1536, 512)
+    zeros("tab", 2048, TAB - 2048)
 
     iota(r("ic", 0, 256), [[32, 4], [128, 2], [1, 32]], 0, 0)
-    iota(r("dg", 0, 512), [[0, 512]], 0, 0)
     iota(r("pat", 0, 256), [[0, 8], [-2, 16], [-32, 2]], 256, 0)
+    iota(r("ht", 0, 512), [[0, 512]], 0, 0)
     iota(r("posc", 256, 768), [[1, 512]], 257, 0)
     iota(r("loc", base, base + P), [[1, P]], 0, 0)
-    iota(r("ht", 0, 512), [[0, 512]], 0, 0)
 
     tab = r("tab", 0, TAB)
     for b in range(4):
@@ -309,26 +297,26 @@ def rank_program(g, core, T, topo):
         act(r("hm", 64 * b, 64 * b + 64), r("hma", 0, 64), Fn.Copy, bias=1024.0, scale=-66560.0)
     for b in range(4):
         mm("dec", b, 256, "eq", 128 * b, "qx", 0)
-        act(r("own", 256 * b, 256 * b + 256), r("dec", 512 * b, 512 * b + 256), Fn.Copy)
+        act(r("own", STR * b + OFF, STR * b + STR), r("dec", 512 * b, 512 * b + 256), Fn.Copy)
     op("v", lambda: g.vector.tensor_copy(T.nboi[:, 0:16], T.nbw[:, 0:64].indirect(T.nbof[:, 0:1])), [r("nbw", 0, 64), r("nbof", 0, 1)], [r("nboi", 0, 16)])
-    scatter(tab, r("my0", 0, 2), r("posc", 224, 256))
     nbi, nbo, nb3 = r("nboi", 0, 8), r("nbo", 0, 8), r("nb3", 0, 8)
+    ts(cf(21), cf(3), -2.0, Op.mult, cf(2), Op.add)
+    ts(cf(22), cf(4), -2.0, Op.mult, cf(2), Op.add)
     ts(r("nbsh", 0, 8), nbi, 8, Op.arith_shift_right)
     cp(nbo, nbi)
-    gather(r("olk", 0, 32), tab, r("oix", 0, 2))
+    scatter(tab, r("my0", 0, 2), r("posc", 224, 256))
     ts(r("nba", 0, 8), r("nbsh", 0, 8), float(STR - P), Op.mult, float(OFF - NONE), Op.add)
     ts(r("nbn", 0, 8), nbo, 0.0, Op.is_lt, float(NONE + 1 + STR - P - OFF), Op.mult)
+    gather(r("olk", 0, 32), tab, r("oix", 0, 2))
 
     def run_on(out, a, width):
         scan(out, r("hm", 0, width), a, 0.0, Op.add, Op.max)
 
-    run_on(r("ofl", 0, 32), r("olk", 0, 32), 32)
     tt(r("nba", 0, 8), r("nba", 0, 8), nbo, Op.add)
-    ts(cf(21), cf(3), -2.0, Op.mult, cf(2), Op.add)
-    ts(r("tk0", 0, 2), r("ofl", 15, 32, st=16), cf(19), Op.subtract, 0.0, Op.is_gt)
-    tt(r("nbm", 0, 8), r("nba", 0, 8), r("nbn", 0, 8), Op.add)
-    ts(cf(22), cf(4), -2.0, Op.mult, cf(2), Op.add)
     ts(cf(23), cf(4), -2.0, Op.mult, cf(21), Op.add)
+    run_on(r("ofl", 0, 32), r("olk", 0, 32), 32)
+    tt(r("nbm", 0, 8), r("nba", 0, 8), r("nbn", 0, 8), Op.add)
+    ts(r("tk0", 0, 2), r("ofl", 15, 32, st=16), cf(19), Op.subtract, 0.0, Op.is_gt)
 
     def settle(first):
         if first:
@@ -339,31 +327,40 @@ def rank_program(g, core, T, topo):
         for h in (0, 1):
             ts(r("nbu", 4 * h, 4 * h + 4), r("nbm", 4 * h, 4 * h + 4), r("nf", h, h + 1), Op.mult, float(NONE), Op.add)
 
-    def masks(t):
-        scatter(tab, r("land%d" % t, 0, 14), r("posc", P * t, P * t + 224))
+    def masks(t, f):
+        scatter(tab, r("lnr%d" % t, 0, 2), r("posc", P * t + 192, P * t + 224))
+        f[0]()
+        scatter(tab, r("land%d" % t, 0, 12), r("posc", P * t, P * t + 192))
+        f[1]()
         gather(r("lk", 0, 128), tab, r("nbu", 0, 8))
+        f[2]()
         run_on(r("pv", 0, 128), r("lk", 0, 128), 128)
+        f[3]()
         ts(r("zo", 0, 8), r("pv", 15, 128, st=16), cf(19), Op.subtract)
         ts(r("zf", 0, 8), r("pv", 15, 128, st=16), cf(19), Op.subtract, -1.0, Op.add)
 
+    fill(r("ones", 0, 2), 1.0)
+    ts(r("negm", 0, 64), r("c16", 0, 64), cf(1), Op.not_equal, LOW, Op.mult)
     settle(True)
+    for b in range(4):
+        zeros("own", STR * b, OFF)
     for d, b in enumerate((2, 21, 22, 23)):
         act(r("plm", 64 * d, 64 * d + 64), r("ic", 64 * d, 64 * d + 64), Fn.Identity, bias=cf(b))
     for h in (0, 1):
         act(r("ed", 512 * h + 1, 512 * h + 512, st=2), r("plm", 0, 256), Fn.Identity, bias=r("cf", 12 + h, 13 + h), scale=2.0 ** -120)
-    masks(0)
-    fill(r("ones", 0, 2), 1.0)
-    for h in (0, 1):
+
+    def lows(h):
         fill(r("zsb", ZW * h, ZW * h + 1), LOW)
         fill(r("gs", 96 * h + 64, 96 * h + 96), LOW)
-    ts(r("negm", 0, 64), r("c16", 0, 64), cf(1), Op.not_equal, LOW, Op.mult)
-    ts(r("segm", 0, 64), r("c16", 0, 64), 0.0, Op.is_equal, LOW, Op.mult)
 
     def digits(h):
         ts(r("dg", 16 + h, 23 + h, st=6), r("ones", 0, 2), cf(2), Op.mult, float(OFF + 16 + 128 * h), Op.add)
         ts(r("dg", 48 + 6 * h, 50 + 6 * h), r("ones", 0, 2), cf(0), Op.mult, -16.0, Op.add)
 
     digits(0)
+    digits(1)
+    masks(0, [lambda: lows(0), lambda: lows(1), lambda: quant("dpq", "dpqs", 0, 128, "dg", 0, 512),
+              lambda: ts(r("segm", 0, 64), r("c16", 0, 64), 0.0, Op.is_equal, LOW, Op.mult)])
 
     def move(e, out, a):
         if e == "v":
@@ -375,12 +372,19 @@ def rank_program(g, core, T, topo):
         c = "comb%d" % t
         more = t < R - 1
         zs = lambda h, a, w: r("zsb", ZW * h + 1 + P * t + a, ZW * h + 1 + P * t + a + w)
+        keep = lambda b: act(r("par", PW * b + P * t, PW * b + P * t + P), r("dec", 512 * b, 512 * b + P), Fn.Copy)
         for h in (0, 1):
-            mm("zz", 2 + h, 128, "qx", 128 * h, c, P * t + 192)
+            mm("zz", 2 + h, 128, "qx", 128 * h, c, 192)
             act(zs(h, 192, 64), r("zz", 1024 + 512 * h, 1088 + 512 * h), Fn.Copy)
         for h in (0, 1):
-            mm("zz", h, 192, "qx", 128 * h, c, P * t)
-            act(zs(h, 0, 192), r("zz", 512 * h, 512 * h + 192), Fn.Copy)
+            mm("zz", h, 128, "qx", 128 * h, c, 0)
+            act(zs(h, 0, 128), r("zz", 512 * h, 512 * h + 128), Fn.Copy)
+        for h in (0, 1):
+            mm("zz", 2 + h, 128, "qx", 128 * h, c, 128)
+            act(zs(h, 128, 64), r("zz", 1024 + 512 * h, 1088 + 512 * h), Fn.Copy)
+        for b in range(4):
+            mm("dec", b, P, "eq", 128 * b, c, 0)
+        keep(0)
 
         def scores(h):
             w, o, q = r("zsb", ZW * h, ZW * h + 1 + P * t + P), r("zo", 4 * h, 4 * h + 4), r("gs", 96 * h, 96 * h + 64)
@@ -389,34 +393,28 @@ def rank_program(g, core, T, topo):
         def own_scores(h):
             scan(r("sbx", 64 * h, 64 * h + 64), r("segm", 0, 64), r("gs", 96 * h, 96 * h + 64), LOW, Op.add, Op.max)
 
+        def best(h):
+            a = r("gs", 96 * h, 96 * h + 96)
+            scan(r("sc", 96 * h, 96 * h + 96), a, a, LOW, Op.max, Op.max)
+
         sb = lambda h: r("sbx", 15 + 64 * h, 64 + 64 * h, st=16)
         bst = lambda h: r("sc", 96 * h + 95, 96 * h + 96)
         k4 = lambda name, h: r(name, 4 * h, 4 * h + 4)
         isbest = lambda h: ts(k4("e8", h), sb(h), bst(h), Op.is_equal)
+        turn = lambda h: tr(r("row", 32 * h, 32 * h + 32), r("sc", 96 * h + 64, 96 * h + 96))
         scores(0)
-        if t == 0:
-            digits(1)
         scores(1)
-        for h in (0, 1):
-            a = r("gs", 96 * h, 96 * h + 96)
-            scan(r("sc", 96 * h, 96 * h + 96), a, a, LOW, Op.max, Op.max)
-        for h in (0, 1):
-            tr(r("row", 32 * h, 32 * h + 32), r("sc", 96 * h + 64, 96 * h + 96))
-        if more:
-            lst = []
-            for t2 in range(t + 1, R):
-                lst += copies(c, P * t, "comb%d" % t2, P * t, P)
-            if t == 0:
-                lst += copies("qx", 0, "finw", 0, P)
-            dmas("dc%d" % t, lst)
+        best(0)
+        best(1)
+        turn(0)
         own_scores(0)
+        turn(1)
+        own_scores(1)
         for b in range(4):
             move("v" if b < 2 else "s", r("row", 64, 128, 32 * b, 32 * b + 32), r("row", 0, 64, 32 * (b ^ 1), 32 * (b ^ 1) + 32))
-        own_scores(1)
+        isbest(0)
         for b in (0, 1):
             move("v" if b < 1 else "s", r("row", 128, 256, 64 * b, 64 * b + 64), r("row", 0, 128, 64 * (1 - b), 64 * (1 - b) + 64))
-        isbest(0)
-        isbest(1)
 
         def differ(e, h, i):
             a, o = r("row", 128 * i, 128 * i + 128), r("ed", 512 * h + 256 * i, 512 * h + 256 * i + 256, st=2)
@@ -426,12 +424,10 @@ def rank_program(g, core, T, topo):
                 act(o, a, Fn.Identity, bias=bst(h), scale=-1.0)
 
         differ("v", 0, 0)
-        tt(r("t8", 0, 8), r("e8", 0, 8), r("zf", 0, 8), Op.mult)
-        differ("s", 0, 1)
         differ("s", 1, 0)
+        differ("s", 0, 1)
         differ("s", 1, 1)
-        for h in (0, 1):
-            act(k4("ne8", h), sb(h), Fn.Sign, bias=bst(h), scale=-1.0)
+        isbest(1)
 
         def ahead(x, w):
             scan(r("cm", x, x + w), r("ste", 0, w), r("ed", x, x + w), 0.0, Op.mult, Op.add)
@@ -439,96 +435,122 @@ def rank_program(g, core, T, topo):
         def count(h):
             act(r("sg", 256 * h, 256 * h + 256), r("cm", 512 * h + 1, 512 * h + 512, st=2), Fn.Sign, accum=r("rs", h, h + 1))
 
-        ahead(0, 256)
-        ahead(256, 256)
-        count(0)
-        ahead(512, 512)
-        count(1)
-        scan(r("sf", 0, 8), r("ne8", 0, 8), r("t8", 0, 8), 0.0, Op.mult, Op.add)
-        ts(r("val", 0, 2), r("sc", 95, 192, st=96), -1e29, Op.is_gt)
-        loc2 = r("sf", 3, 8, st=4)
-        top = 8 if t == 2 else 0
-        ts(r("hi", 0, 2), loc2, 1.0 / 32, Op.mult)
-
         def slots(h):
             ts(r("oh", h, 512, st=2), r("pat", 0, 256), r("rs", h, h + 1), Op.is_equal, r("val", h, h + 1), Op.mult)
 
+        ahead(0, 256)
+        ahead(256, 256)
+        count(0)
+        ahead(512, 256)
+        ahead(768, 256)
+        count(1)
+        ts(r("val", 0, 2), r("sc", 95, 192, st=96), -1e29, Op.is_gt)
+        tt(r("t8", 0, 8), r("e8", 0, 8), r("zf", 0, 8), Op.mult)
+        ts(r("ne8", 0, 8), r("e8", 0, 8), -1.0, Op.mult, 1.0, Op.add)
         slots(0)
-        ts(r("hf", 0, 2), r("hi", 0, 2), 32.0, Op.mult)
+        scan(r("sf", 0, 8), r("ne8", 0, 8), r("t8", 0, 8), 0.0, Op.mult, Op.add)
+        loc2 = r("sf", 3, 8, st=4)
+        top = 8 if t == 2 else 0
+        slots(1)
+        ts(r("hf", 0, 2), loc2, STEP32, Op.add, STEP32, Op.subtract)
+        quant("ohq", "ohqs", 0, 128, "oh", 0, 512)
+        mm("zz", 2, 128, "ohq", 0, "dpq", 0)
+        keep(1)
         for u in (0, 1):
             act(r("dg", 6 * u, 6 * u + 2), r("hf", 0, 2), Fn.Copy, bias=-32.0 * top)
             tt(r("dg", 32 + 6 * u, 34 + 6 * u), loc2, r("hf", 0, 2), Op.subtract)
-        slots(1)
+        keep(2)
         quant("dgq", "dgqs", 0, 128, "dg", 0, 512)
-        quant("ohq", "ohqs", 0, 128, "oh", 0, 512)
-        mm("zz", 2, 128, "ohq", 0, "dgq", 0)
-        if t == 0:
-            ts(nb3, nbo, 1.0, Op.add)
-        ts(r("tk", 0, 1), r("rs", 0, 1), 193.0, Op.is_gt, r("val", 0, 1), Op.mult)
-        ts(r("tk", 1, 2), r("rs", 1, 2), 193.0, Op.is_gt, r("val", 1, 2), Op.mult)
-        tt(r("u8", 0, 8), r("e8", 0, 8), nb3, Op.mult)
-        scan(r("sn", 0, 8), r("ne8", 0, 8), r("u8", 0, 8), 0.0, Op.mult, Op.add)
+        mm("zz", 3, 128, "ohq", 0, "dgq", 0)
         out = lambda i: r("zz", 1024 + i, 1025 + i)
-        for u in (0, 1):
-            ts(r("offp", u, u + 1), out(u), out(8 + u), Op.add, 32.0 * top, Op.add)
         for u, k in enumerate((1, 25)):
             ts(r("pl", u, u + 1), out(4 + u), out(12 + u), Op.add, cf(k), Op.max)
-        pick("pk", 0, c, P * t + P, "offp", 0, 2)
-        ts(r("offo", 0, 2), r("pl", 0, 2), -float(OFF), Op.add, 0.0, Op.max)
-        for b in range(4):
-            gather_s(r("od", 32 * b, 32 * b + 32), r("own", 256 * b, 256 * b + 256), r("offo", 0, 2))
+        keep(3)
+        ts(r("tk", 0, 1), r("rs", 0, 1), 193.0, Op.is_gt, r("val", 0, 1), Op.mult)
         my = "my%d" % (t + 1)
-        ts(r(my, 0, 2), r("pl", 0, 2), float(STR * rank), Op.add)
+        lv = P - 1 + S * t
+        located = lambda: scatter(r("loc", base - OFF, base + P), r("pl", 0, 2), r("posc", lv, lv + S))
+        if more:
+            ts(r(my, 0, 2), r("pl", 0, 2), float(STR * rank), Op.add)
+        else:
+            located()
+        for b in range(4):
+            gather_s(r("od", 32 * b, 32 * b + 32), r("own", STR * b, STR * b + STR), r("pl", 0, 2))
         if more:
             send_list(t + 1)
+        for u in (0, 1):
+            ts(r("offp", u, u + 1), out(512 + u), out(520 + u), Op.add, 32.0 * top, Op.add)
+        ts(r("tk", 1, 2), r("rs", 1, 2), 193.0, Op.is_gt, r("val", 1, 2), Op.mult)
 
-        def parents():
-            if t == 0:
-                ts(r("z2", 0, 2), place2, float(P * rank + 1), Op.add)
-                tt(r("w3", 0, 2), r("z2", 0, 2), r("tk0", 0, 2), Op.mult)
-                ts(r("pa2", 0, 2), r("w3", 0, 2), -1.0, Op.add)
-            tt(r("y2", 0, 2), r("sn", 3, 8, st=4), r("tk", 0, 2), Op.mult)
-            tt(r("pa2", 0, 2), r("pa2", 0, 2), r("y2", 0, 2), Op.add)
+        def numbers(i):
+            if i == 0:
+                if t == 0:
+                    ts(nb3, nbo, 1.0, Op.add)
+                    ts(r("z2", 0, 2), place2, float(P * rank + 1), Op.add)
+                    tt(r("w3", 0, 2), r("z2", 0, 2), r("tk0", 0, 2), Op.mult)
+                    ts(r("pa2", 0, 2), r("w3", 0, 2), -1.0, Op.add)
+                tt(r("u8", 0, 8), r("e8", 0, 8), nb3, Op.mult)
+            else:
+                scan(r("sn", 0, 8), r("ne8", 0, 8), r("u8", 0, 8), 0.0, Op.mult, Op.add)
 
-        for b in range(4):
-            mm("dec", b, 128, "eq", 128 * b, "pk", 0)
-        lv = P - 1 + S * t
-        scatter(r("loc", 0, TAB), r(my, 0, 2), r("posc", lv, lv + S))
-        if not more:
-            parents()
-            dmas("dpa", [("y", T.pa[0:1, 128 * h:128 * h + 128], T.pa2[:, h:h + 1], [r("pa2", h, h + 1)], []) for h in (0, 1)])
+        def parents(i):
+            if i == 0:
+                tt(r("y2", 0, 2), r("sn", 3, 8, st=4), r("tk", 0, 2), Op.mult)
+            else:
+                tt(r("pa2", 0, 2), r("pa2", 0, 2), r("y2", 0, 2), Op.add)
+
         half_row = lambda m: run_on(r("flx", 128 * m, 128 * m + 128), r("loc", base + 128 * m, base + 128 * m + 128), 128)
         half_list = lambda m: ts(r("fo", 8 * m, 8 * m + 8), r("flx", 128 * m + 15, 128 * m + 128, st=16), cf(19), Op.subtract)
+
+        def blend(b):
+            w, o, a, q = r("par", PW * b, PW * b + P * t + P), r("offp", 0, 2), r("od", 32 * b, 32 * b + 32), r("ht", b, 128, st=4)
+            op("v", lambda: g.vector.tensor_tensor(ap(q), ap(w).indirect(ap(o)), ap(a), Op.add), [w, o, a], [q])
+
+        def y_of(cq, a):
+            for o in (0, 1):
+                mm("dec", o, 128, "qw", 128 * o, cq, a)
+                act(r("yb", S * o, S * o + S), r("dec", 512 * o, 512 * o + S), Fn.Copy)
+
+        y_put = lambda o: scatter(r("sy", STR * o, STR * o + STR), r("pl", 0, 2), r("yb", S * o, S * o + S))
+
         for b in range(4):
-            tt(r("ht", b, 128, st=4), r("dec", 512 * b, 512 * b + 32), r("od", 32 * b, 32 * b + 32), Op.add)
-            if not more and b < 2:
-                half_row(b)
-            elif not more:
-                half_list(b - 2)
+            blend(b)
         if more:
-            d, o = "comb%d" % (t + 1), P * (t + 1) + 224
+            d, o = "comb%d" % (t + 1), 224
             quant(d, d + "s", o, o + 128, "ht", 0, 512)
             send_cols(t + 1)
             dmas("df%d" % t, copies(d, o, "finw", P + S * t, S))
-            scatter(tab, r(my, 0, 2), r("posc", P * (t + 1) + 224, P * (t + 1) + 256))
-            settle(False)
-            masks(t + 1)
-            parents()
             if t == 0:
                 quant("qw", "qws", 0, 256, "wt", 0, 1024)
+                for u in (0, 1):
+                    mm("zz", u, 256, "qw", 128 * u, "qx", 0)
+                    act(r("sy", STR * u + OFF, STR * u + STR), r("zz", 512 * u, 512 * u + 256), Fn.Copy)
+            numbers(0)
+            y_of(d, o)
+            scatter(tab, r(my, 0, 2), r("posc", P * (t + 1) + 224, P * (t + 1) + 256))
+            settle(False)
+            masks(t + 1, [located, lambda: numbers(1), lambda: parents(0), lambda: parents(1)])
+            y_put(0)
+            y_put(1)
         else:
+            half_row(0)
             quant("finw", "finws", 320, 448, "ht", 0, 512)
+            y_of("finw", 320)
+            half_row(1)
+            half_list(0)
+            numbers(0)
+            half_list(1)
+            numbers(1)
+            pick("fin", 0, "finw", 352, "fo", 0, 16)
+            y_put(0)
+            y_put(1)
+            parents(0)
+            parents(1)
 
-    for m in (0, 1):
-        pick("fin", 128 * m, "finw", 352, "fo", 8 * m, 8 * m + 8)
-        for o in (0, 1):
-            mm("zz", 2 * m + o, 128, "qw", 128 * o, "fin", 128 * m)
-    for m in (0, 1):
-        cp(r("sy", 128 * m, 128 * m + 128), r("zz", 1024 * m, 1024 * m + 128))
-        act(r("sy", 256 + 128 * m, 384 + 128 * m), r("zz", 1024 * m + 512, 1024 * m + 640), Fn.Copy)
     dmas("dout", [("y", T.oc[:], T.fin[:].bitcast(dt.uint8), [r("fin", 0, 256)], [])] +
-         [("y", T.osc[4 * k:4 * k + 4, :], T.fins[32 * k:32 * k + 4, :], [r("fins", 0, 256)], []) for k in range(4)] +
-         [(q, T.y[:, 256 * o:256 * o + 256], T.sy[:, 256 * o:256 * o + 256], [r("sy", 256 * o, 256 * o + 256)], []) for o, q in enumerate("ys")])
+         [("s", T.osc[4 * k:4 * k + 4, :], T.fins[32 * k:32 * k + 4, :], [r("fins", 0, 256)], []) for k in range(4)] +
+         [("y", T.y[:, 256 * o:256 * o + 256], T.sy[:, STR * o + OFF:STR * o + STR], [r("sy", STR * o, STR * o + STR)], []) for o in (0, 1)])
+    dmas("dpa", [("s", T.pa[0:1, 128 * h:128 * h + 128], T.pa2[:, h:h + 1], [r("pa2", h, h + 1)], []) for h in (0, 1)])
     for sem in cnt:
         if known["g"].get(sem, 0) < cnt[sem]:
             g.wait_ge(T.sem[sem], cnt[sem])

@@ -3,33 +3,30 @@ from concourse.bass import DstId, RemoteDMATransfer
 from concourse.mybir import dt, AluOpType as Op, AxisListType, ActivationFunctionType as Fn
 
 F8 = "float8_e4m3fn_x4"
-WC, WF = 384, 448
+CW = 384
 STR, OFF = 304, 48
-TAB, NONE = 2440, 2432
-ZW = 776
+TAB = 8 * STR
 PW = 768
-STEP32 = 1.5 * 2.0 ** 28
-LOW = -9e29
+HT = 128
+STEP64, STEP2K = 1.5 * 2.0 ** 29, 1.5 * 2.0 ** 34
+LOW, TINY = -2.0 ** 99, 2.0 ** -100
 SCRATCH = {"dec": ("psum", [128, 2048], "float32"), "zz": ("psum", [128, 2048], "float32")}
-for _n, _w in (("qx", 256), ("qw", 256), ("eq", 512), ("comb0", WC), ("comb1", WC), ("comb2", WC), ("finw", WF), ("fin", 256),
-               ("ohq", 128), ("dgq", 128), ("dpq", 128)):
+for _n, _w in (("big", 256 + 3 * CW), ("qw", 256), ("eq", 512), ("comb0", 256), ("fin", 256), ("ohq", 138)):
     SCRATCH[_n] = ("sbuf", [128, _w], F8)
     SCRATCH[_n + "s"] = ("sbuf", [128, _w], "uint8")
-for _d, _l in (("bfloat16", (("xt", 1024), ("wt", 1024), ("half", 128), ("et", 528), ("par", 4 * PW), ("ht", 512), ("own", 4 * STR), ("ste", 512),
-                             ("ed", 1024), ("cm", 1024), ("sg", 512), ("pat", 256), ("oh", 512), ("dg", 512))),
-               ("int32", (("sdw", 2), ("nbw", 64), ("nboi", 16), ("nbsh", 8), ("pint", 1), ("ci", 16))),
-               ("uint16", (("sdu", 2), ("nbof", 2), ("nbu", 8), ("oix", 2), ("my0", 2), ("my1", 2), ("my2", 2), ("land0", 16), ("land1", 16),
-                           ("land2", 16), ("lnr0", 2), ("lnr1", 2), ("lnr2", 2), ("zo", 8), ("pl", 2), ("offp", 2), ("fo", 16))),
-               ("float32", (("yb", 64), ("od", 128), ("nbo", 8), ("nba", 8), ("nbn", 8), ("nbm", 8), ("nb3", 8), ("olk", 32), ("ofl", 32),
-                            ("pidx", 1), ("c16", 64), ("ic", 256), ("cf", 32), ("plm", 256), ("ones", 2), ("posc", 768), ("tab", TAB),
-                            ("loc", TAB), ("hma", 64), ("hm", 128), ("negm", 64), ("segm", 64), ("lk", 128), ("pv", 128), ("zf", 8),
-                            ("zsb", 2 * ZW), ("gs", 192), ("sc", 192), ("sbx", 128), ("row", 256), ("e8", 8), ("ne8", 8), ("t8", 8),
-                            ("u8", 8), ("sf", 8), ("sn", 8), ("val", 2), ("rs", 2), ("y2", 2), ("z2", 2), ("hf", 2), ("tk0", 2),
-                            ("tk", 2), ("nf", 2), ("pa2", 2), ("w3", 2), ("flx", 256), ("sy", 2 * STR)))):
+for _d, _l in (("bfloat16", (("xt", HT + 1024), ("wt", 1024), ("half", 256), ("et", 528), ("par", 4 * PW), ("own", 4 * STR), ("fl", 512),
+                             ("cn", 256), ("pat", 256), ("oh", 552))),
+               ("int32", (("sdw", 2), ("nbw", 64), ("nbi", 8), ("nbsh", 8), ("pint", 1), ("ci", 8))),
+               ("uint16", (("sdu", 2), ("nbu", 8), ("rep", 8), ("oix", 2), ("my0", 2), ("my1", 2), ("my2", 2), ("land0", 16), ("land1", 16),
+                           ("land2", 16), ("lnr0", 2), ("lnr1", 2), ("lnr2", 2), ("zo", 8), ("pl", 6), ("offp", 2), ("fo", 16))),
+               ("float32", (("yb", 192), ("od", 128), ("nba", 8), ("nbt", 8), ("b8", 8), ("pr", 8), ("olk", 32), ("ofl", 32), ("place", 2),
+                            ("c16", 128), ("c32", 32), ("k4", 4), ("k2", 2), ("cf", 16), ("posc", 768), ("lv", 96), ("tab", TAB), ("loc", STR),
+                            ("hm", 128), ("negm", 128), ("segm", 128), ("bs", 128), ("lk", 128), ("pv", 128), ("zsb", 2 + 2 * PW),
+                            ("gs", 128), ("sc", 128), ("ne", 128), ("sl", 128), ("row", 256), ("df", 64), ("thr", 32), ("pen", 2),
+                            ("a2", 4), ("b2", 4), ("tk", 8), ("pk", 8), ("pz", 8), ("pa2", 2), ("flx", 256), ("sy", 2 * STR)))):
     for _n, _w in _l:
         SCRATCH[_n] = ("sbuf", [128, _w], _d)
-SEMAPHORES = ["v", "s", "p", "gp", "dsd", "dx", "dnb", "dw", "arl0", "arl1", "arl2", "arm0", "arm1", "arm2", "arc0", "arc1", "arc2",
-              "ard0", "ard1", "ard2", "arn0", "arn1", "arn2", "dc0", "df0", "df1", "di", "dout", "dpa", "sent"]
+SEMAPHORES = ["v", "s", "p", "gp", "dsd", "dx", "dnb", "dw", "dout", "dpa", "sent"] + ["ar%s%d" % (_x, _t) for _x in "lmsfcdn" for _t in range(3)]
 
 
 def r(name, c0, c1, p0=0, p1=128, st=1):
@@ -108,6 +105,8 @@ def rank_program(g, core, T, topo):
 
     def ap(q):
         name, c0, c1, p0, p1, st = q
+        if st < 0:
+            return T[name][p0:p1, c1 - 1:(c0 - 1 if c0 else None):st]
         return T[name][p0:p1, c0:c1] if st == 1 else T[name][p0:p1, c0:c1:st]
 
     def tup(*xs):
@@ -132,7 +131,7 @@ def rank_program(g, core, T, topo):
         op("v", lambda: g.vector.transpose(ap(out), ap(a)), [a], [out])
 
     def scan(out, a, b, init, o0, o1):
-        op("v", lambda: g.vector.tensor_tensor_scan(ap(out), ap(a), ap(b), init, o0, o1), [a, b], [out])
+        op("v", lambda: g.vector.tensor_tensor_scan(ap(out), ap(a), ap(b), sv(init), o0, o1), [a, b] + tup(init), [out])
 
     def fill(out, c):
         op("v", lambda: g.vector.memset(ap(out), c), [], [out])
@@ -143,16 +142,18 @@ def rank_program(g, core, T, topo):
         else:
             op("g", lambda: g.iota(ap(out), pattern, base, cm), [], [out])
 
-    def act(out, a, func, bias=0.0, scale=1.0, accum=None):
-        w = [out] + tup(accum)
-        op("s", lambda: g.scalar.activation(ap(out), ap(a), func, bias=sv(bias), scale=sv(scale), accum_out=None if accum is None else ap(accum)),
-           [a] + tup(bias, scale), w)
+    def act(out, a, func=Fn.Copy, bias=0.0, scale=1.0):
+        op("s", lambda: g.scalar.activation(ap(out), ap(a), func, bias=sv(bias), scale=sv(scale)), [a] + tup(bias, scale), [out])
 
-    def quant(c, s, a, b, src, x0, x1):
+    def quant(c, a, b, src, x0, x1):
+        s = c + "s"
         op("v", lambda: g.vector.quantize_mx(T[c][:, a:b], T[s][:, a:b], T[src][:, x0:x1]), [r(src, x0, x1)], [r(c, a, b), r(s, a, b)])
 
     def gather(out, win, off):
         op("v", lambda: g.vector.tensor_copy(ap(out), ap(win).indirect(ap(off))), [win, off], [out])
+
+    def gather_add(out, win, off, b):
+        op("v", lambda: g.vector.tensor_tensor(ap(out), ap(win).indirect(ap(off)), ap(b), Op.add), [win, off, b], [out])
 
     def gather_s(out, win, off):
         op("s", lambda: g.scalar.activation(ap(out), ap(win).indirect(ap(off)), Fn.Copy), [win, off], [out])
@@ -174,27 +175,23 @@ def rank_program(g, core, T, topo):
            [r(c1, a1, a1 + 128), r(c1 + "s", a1, a1 + 128), r(c2, a2, a2 + width), r(c2 + "s", a2, a2 + width)],
            [r(out, 512 * bank, 512 * bank + 512)])
 
-    far = [q for q in range(n) if topo.chip(cores[q]) != topo.chip(core)]
-    near = [q for q in range(n) if q != rank and topo.chip(cores[q]) == topo.chip(core)]
     mate = rank ^ 1
-    assert near == [mate]
+    assert topo.chip(cores[mate]) == topo.chip(core)
+    far = [q for q in range(n) if topo.chip(cores[q]) != topo.chip(core)]
+    level = sorted((q for q in far if topo.die(cores[q]) == topo.die(core)), key=lambda q: q ^ rank)
+    cross = [q ^ 1 for q in level]
+    block = (cross[::-1] + level[::-1] + [mate, rank]).index
     fe = topo.engines(core, cores[far[0]])
-    ne = [e for e in topo.engines(core, cores[mate]) if e not in fe][::2]
-    block = lambda q: n - 1 - (q ^ rank)
-    far.sort(key=block)
+    ne = [e for e in topo.engines(core, cores[mate]) if e not in fe]
+    fresh = lambda t: ("comb0", 0) if t == 0 else ("big", P + CW * (t - 1))
 
-    def dest(q):
-        a = topo.addr(cores[q])
-        return DstId(rid=a[0], pnc=a[1])
-
-    def send(fsem, nsem, src, dst_of, reads, fars=far, nears=near):
+    def send(reads, parts):
         before("g", reads, [])
         out = []
-        for qs, es, sem in ((fars, fe, fsem), (nears, ne, nsem)):
-            if not qs:
-                continue
-            out.append(RemoteDMATransfer(dst_ids=[dest(q) for q in qs], dma_engine_mask=sum(1 << e for e in es), remote_sem=T.sem[sem],
-                                         srcs=[src], dsts=[dst_of(q) for q in qs], alu_op=0))
+        for es, sem, src, to in parts:
+            ids = [topo.addr(cores[q]) for q, d in to]
+            out.append(RemoteDMATransfer(dst_ids=[DstId(rid=a[0], pnc=a[1]) for a in ids], dma_engine_mask=sum(1 << e for e in es),
+                                         remote_sem=T.sem[sem], srcs=[src], dsts=[d for q, d in to], alu_op=0))
             cnt["sent"] = cnt.get("sent", 0) + len(es)
         g.remote_dma_fused(out, local_sem=T.sem["sent"])
 
@@ -205,352 +202,290 @@ def rank_program(g, core, T, topo):
             note("far", [], [a], (sem, total, {}, seq[0]))
 
     def send_list(t):
-        to = lambda q: T["lnr%d" % t][:, 0:2] if q == mate else T["land%d" % t][:, 2 * block(q):2 * block(q) + 2]
-        send("arl%d" % t, "arm%d" % t, T["my%d" % t][:, 0:2], to, [r("my%d" % t, 0, 2)])
+        src, to = T["my%d" % t][:, 0:2], lambda q: (q, T["land%d" % t][:, 2 * block(q):2 * block(q) + 2])
+        send([r("my%d" % t, 0, 2)], [(fe, "arl%d" % t, src, [to(q) for q in far]), (ne, "arm%d" % t, src, [(mate, T["lnr%d" % t][:, 0:2])])])
         landed("arm%d" % t, len(ne), [r("lnr%d" % t, 0, 2)])
         landed("arl%d" % t, len(fe) * len(far), [r("land%d" % t, 0, 12)])
 
-    def send_cols(t):
-        c, fs, nr = "comb%d" % t, "arc%d" % t, "arn%d" % t
-        o, w = 224, 192
-        send(fs, nr, T[c][:, o:o + S].bitcast(dt.uint8), lambda q: T[c][:, S * block(q):S * block(q) + S].bitcast(dt.uint8), [r(c, o, o + S)])
-        to = lambda q: T[c + "s"][:, S * block(q):S * block(q) + S]
-        send(fs, nr, T[c + "s"][:, o:o + S], to, [r(c + "s", o, o + S)], far[:4])
-        send("ard%d" % t, nr, T[c + "s"][:, o:o + S], to, [r(c + "s", o, o + S)], far[4:], [])
-        landed(nr, 2 * len(ne), [r(c, w, w + S), r(c + "s", w, w + S)])
-        landed(fs, len(fe) * (len(far) + 4), [r(c, 0, w), r(c + "s", 0, 4 * S)])
-        landed("ard%d" % t, len(fe) * (len(far) - 4), [r(c + "s", 4 * S, w)])
-
-    def copies(src, s0, dst, d0, w):
-        return [("y", T[dst][:, d0:d0 + w].bitcast(dt.uint8), T[src][:, s0:s0 + w].bitcast(dt.uint8), [r(src, s0, s0 + w)], [r(dst, d0, d0 + w)]),
-                ("y", T[dst + "s"][:, d0:d0 + w], T[src + "s"][:, s0:s0 + w], [r(src + "s", s0, s0 + w)], [r(dst + "s", d0, d0 + w)])]
+    def send_cols(t, meanwhile):
+        c, a = fresh(t)
+        s = c + "s"
+        sc = lambda i, k=1: T[s][:, a + S * i:a + S * (i + k)]
+        co = lambda i: T[c][:, a + S * i:a + S * i + S].bitcast(dt.uint8)
+        at = lambda name, i, k=1: r(name, a + S * i, a + S * (i + k))
+        ars, arf, arc, ard, arn = ["ar%s%d" % (x, t) for x in "sfcdn"]
+        send([at(s, 7)], [(fe, ars, sc(7), [(q, sc(block(q))) for q in level]), (ne, arn, sc(7), [(mate, sc(6))])])
+        send([at(c, 7)], [(fe, arf, co(7), [(level[0], co(5))]), (ne, arn, co(7), [(mate, co(6))])])
+        send([at(c, 7)], [(fe, arc, co(7), [(level[1], co(4))])])
+        rest = level[2:] + cross[1:]
+        send([at(c, 7)], [(fe, ard, co(7), [(q, co(block(q))) for q in rest])])
+        landed(arn, 2 * len(ne), [at(c, 6), at(s, 6)])
+        landed(ars, 3 * len(fe), [at(s, 3, 3)])
+        landed(arf, len(fe), [at(c, 5)])
+        landed(arc, len(fe), [at(c, 4)])
+        meanwhile()
+        send([at(s, 3, 3)], [(ne, ard, sc(3, 3), [(mate, sc(0, 3))])])
+        send([at(c, 5)], [(ne, ard, co(5), [(mate, co(2))])])
+        landed(ard, len(fe) * len(rest) + 2 * len(ne), [at(c, 0, 4), at(s, 0, 3)])
 
     dmas("dsd", [(q, T.sdw[16 * a:16 * a + 16, :], T.sd[:], [], [r("sdw", 0, 2, 16 * a, 16 * a + 16)]) for a, q in enumerate("ysys")])
-    dmas("dx", [("y", T.xt[:], T.x[:], [], [r("xt", 0, 1024)])])
-    dmas("dnb", [("y", T.nbw[16 * a:16 * a + 16, :], T.nb[:], [], [r("nbw", 0, 64, 16 * a, 16 * a + 16)]) for a in range(8)])
+    dmas("dx", [("y", T.xt[:, HT:], T.x[:], [], [r("xt", HT, HT + 1024)])])
+    dmas("dnb", [("y", T.nbw[16 * a:16 * a + 16, 0:57], T.nb[:, a:a + 57], [], [r("nbw", 0, 57, 16 * a, 16 * a + 16)]) for a in range(8)])
     dmas("dw", [("y", T.wt[:], T.w[:], [], [r("wt", 0, 1024)])])
 
     base = STR * rank + OFF
-    pint, pidx = r("pint", 0, 1), r("pidx", 0, 1)
+    pint, place = r("pint", 0, 1), r("place", 0, 2)
     iota(pint, [[0, 1]], 0, 1, False)
-    iota(pidx, [[0, 1]], 0, 1)
-    iota(r("posc", 0, 256), [[1, 256]], 1, 0)
+    iota(place, [[128, 2]], 0, 1)
     ci = lambda i: r("ci", i, i + 1)
     cf = lambda i: r("cf", i, i + 1)
-    fill(r("ste", 0, 512, st=2), 0.0)
-    fill(r("ste", 1, 512, st=2), 1.0)
+    fill(r("half", 0, 256), 0.5)
+    fill(r("et", 0, 528), 0.0)
 
     def zeros(name, a, w):
-        act(r(name, a, a + w), r("ste", 0, w), Fn.Copy, scale=0.0)
+        act(r(name, a, a + w), r("half", 0, w), scale=0.0)
 
-    for b in range(3):
-        zeros("tab", 512 * b, 512)
-    fill(r("half", 0, 128), 0.5)
-    fill(r("et", 0, 528), 0.0)
+    for b in range(9):
+        zeros("tab", 256 * b, 256)
     e_, h_ = r("et", 3, 515, st=4), r("half", 0, 128)
     op("g", lambda: g.affine_select(ap(e_), ap(h_), [[-1, 128]], Op.is_equal, 0.0, 0, 1), [h_], [e_])
-    ts(ci(7), pint, 4, Op.arith_shift_right)
-    ts(ci(0), pint, 31, Op.bitwise_and)
-    ts(ci(1), pint, 15, Op.bitwise_and)
-    ts(ci(2), pint, 96, Op.bitwise_and)
-    ts(ci(3), pint, 32, Op.bitwise_and)
-    ts(ci(4), pint, 64, Op.bitwise_and)
-    ts(ci(5), pint, 3, Op.bitwise_and)
-    ts(ci(6), pint, 4, Op.bitwise_and)
-    cp(cf(10), pidx)
-    cp(r("cf", 0, 8), r("ci", 0, 8))
+    iota(r("c16", 0, 128), [[0, 8], [1, 16]], 0, 0)
+    for i, m in enumerate((31, 15, 96, 32, 64)):
+        ts(ci(i), pint, m, Op.bitwise_and)
+    ts(r("oix", 0, 2), place, float(base), Op.add)
+    cp(r("cf", 0, 5), r("ci", 0, 5))
 
     for b in range(2):
         ts(r("my0", 0, 2, 64 * b, 64 * b + 64), r("sdw", 0, 2, 0, 64), float(base), Op.add)
     send_list(0)
-    iota(r("c16", 0, 64), [[0, 4], [1, 16]], 0, 0)
+    iota(r("posc", 0, 256), [[2, 256]], 2, 0)
+    iota(r("pr", 0, 8), [[0, 2], [-1, 4]], 3, 0)
     for b in range(2):
         cp(r("sdu", 0, 2, 64 * b, 64 * b + 64), r("sdw", 0, 2, 0, 64))
-    ts(cf(11), pidx, 128.0, Op.add)
-    ts(cf(17), cf(5), -16.0, Op.mult, cf(7), Op.add)
-    fill(r("dg", 0, 512), 0.0)
-    place2 = r("cf", 10, 12)
-    quant("qx", "qxs", 0, 256, "xt", 0, 1024)
-    pick("comb0", 224, "qx", 256, "sdu", 0, 2)
-    send_cols(0)
-    dmas("di", copies("qx", 0, "comb0", 256, 128))
-    dmas("dc0", copies("qx", 0, "finw", 0, P))
-    zeros("tab", 1536, 512)
-    zeros("tab", 2048, TAB - 2048)
+    unpacker = lambda b: quant("eq", 128 * b, 128 * b + 128, "et", 3 - b, 515 - b)
+    for b in range(3):
+        unpacker(b)
+    quant("big", 0, 256, "xt", HT, HT + 1024)
+    ts(cf(5), cf(1), -2048.0, Op.mult, 30720.0, Op.add)
+    pick("comb0", 7 * S, "big", 256, "sdu", 0, 2)
 
-    iota(r("ic", 0, 256), [[32, 4], [128, 2], [1, 32]], 0, 0)
-    iota(r("pat", 0, 256), [[0, 8], [-2, 16], [-32, 2]], 256, 0)
-    iota(r("ht", 0, 512), [[0, 512]], 0, 0)
-    iota(r("posc", 256, 768), [[1, 512]], 257, 0)
-    iota(r("loc", base, base + P), [[1, P]], 0, 0)
+    def small():
+        iota(r("k4", 0, 4), [[3, 2], [0, 2]], -1, 0)
+        iota(r("c32", 0, 32), [[1, 32]], 0, 0)
 
-    tab = r("tab", 0, TAB)
+    send_cols(0, small)
+    unpacker(3)
+    zeros("tab", 256 * 9, TAB - 256 * 9)
+    iota(r("k2", 0, 2), [[16, 2]], 1, 0)
+    iota(r("pat", 0, 256), [[0, 8], [1, 16], [16, 2]], 0, 0)
+    iota(r("posc", 256, 768), [[2, 512]], 514, 0)
+    iota(r("loc", OFF, STR), [[1, P]], 0, 0)
+    iota(r("lv", 0, 96), [[CW, 3], [1, S]], P + 7 * S, 0)
+
+    tab, negm = r("tab", 0, TAB), r("negm", 0, 128)
+    nbi, b8 = r("nbi", 0, 8), r("b8", 0, 8)
+    for k in range(4):
+        cp(r("nbi", 3 - k, 8, st=4), r("nbw", 16 * k, 16 * k + 9, st=8))
+    ts(negm, r("c16", 0, 128), cf(1), Op.not_equal, LOW, Op.mult)
+    act(r("pr", 0, 8), r("pr", 0, 8), scale=2.0 ** 22)
+    act(r("hm", 0, 128), negm, bias=-131072.0, scale=133120.0 / LOW)
     for b in range(4):
-        quant("eq", "eqs", 128 * b, 128 * b + 128, "et", 3 - b, 515 - b)
-    ts(cf(18), cf(6), 2.0, Op.mult, 48.0, Op.add)
-    ts(cf(19), cf(1), -1024.0, Op.mult, 15360.0, Op.add)
-    ts(cf(25), cf(1), 16.0, Op.add)
-    tt(r("nbof", 0, 1), cf(17), cf(18), Op.add)
-    ts(r("oix", 0, 2), place2, float(base), Op.add)
-    ts(r("hma", 0, 64), r("c16", 0, 64), cf(1), Op.is_equal)
-    for b in range(2):
-        act(r("hm", 64 * b, 64 * b + 64), r("hma", 0, 64), Fn.Copy, bias=1024.0, scale=-66560.0)
-    for b in range(4):
-        mm("dec", b, 256, "eq", 128 * b, "qx", 0)
-        act(r("own", STR * b + OFF, STR * b + STR), r("dec", 512 * b, 512 * b + 256), Fn.Copy)
-    op("v", lambda: g.vector.tensor_copy(T.nboi[:, 0:16], T.nbw[:, 0:64].indirect(T.nbof[:, 0:1])), [r("nbw", 0, 64), r("nbof", 0, 1)], [r("nboi", 0, 16)])
-    nbi, nbo, nb3 = r("nboi", 0, 8), r("nbo", 0, 8), r("nb3", 0, 8)
-    ts(cf(21), cf(3), -2.0, Op.mult, cf(2), Op.add)
-    ts(cf(22), cf(4), -2.0, Op.mult, cf(2), Op.add)
+        mm("dec", b, 256, "eq", 128 * b, "big", 0)
+        act(r("own", STR * b + OFF, STR * b + STR), r("dec", 512 * b, 512 * b + 256))
+    ts(r("nbt", 0, 8), nbi, 2048.0, Op.mult, 2048.0 - 770.0, Op.add)
     ts(r("nbsh", 0, 8), nbi, 8, Op.arith_shift_right)
-    cp(nbo, nbi)
     scatter(tab, r("my0", 0, 2), r("posc", 224, 256))
-    ts(r("nba", 0, 8), r("nbsh", 0, 8), float(STR - P), Op.mult, float(OFF - NONE), Op.add)
-    ts(r("nbn", 0, 8), nbo, 0.0, Op.is_lt, float(NONE + 1 + STR - P - OFF), Op.mult)
+    cp(r("rep", 0, 8), r("c16", 0, 8))
+    tt(b8, r("nbt", 0, 8), r("pr", 0, 8), Op.add)
+    ts(r("nba", 0, 8), r("nbsh", 0, 8), float(STR - P), Op.mult, float(OFF), Op.add)
     gather(r("olk", 0, 32), tab, r("oix", 0, 2))
+    gather_add(r("bs", 0, 128), b8, r("rep", 0, 8), negm)
+    tt(r("nbu", 0, 8), r("nba", 0, 8), nbi, Op.add)
 
     def run_on(out, a, width):
         scan(out, r("hm", 0, width), a, 0.0, Op.add, Op.max)
 
-    tt(r("nba", 0, 8), r("nba", 0, 8), nbo, Op.add)
-    ts(cf(23), cf(4), -2.0, Op.mult, cf(21), Op.add)
-    run_on(r("ofl", 0, 32), r("olk", 0, 32), 32)
-    tt(r("nbm", 0, 8), r("nba", 0, 8), r("nbn", 0, 8), Op.add)
-    ts(r("tk0", 0, 2), r("ofl", 15, 32, st=16), cf(19), Op.subtract, 0.0, Op.is_gt)
+    tk = lambda t, h: r("tk", 2 * t + h, 2 * t + h + 1)
+    pk = lambda t, h: r("pk", 2 * t + h, 2 * t + h + 1)
 
-    def settle(first):
-        if first:
-            ts(r("nf", 0, 2), r("tk0", 0, 2), -1.0, Op.mult, 1.0, Op.add)
-            ts(r("cf", 12, 14), place2, -0.5, Op.add, -2.0 ** -120, Op.mult)
-        else:
-            tt(r("nf", 0, 2), r("nf", 0, 2), r("tk", 0, 2), Op.subtract)
+    def settle(t):
         for h in (0, 1):
-            ts(r("nbu", 4 * h, 4 * h + 4), r("nbm", 4 * h, 4 * h + 4), r("nf", h, h + 1), Op.mult, float(NONE), Op.add)
+            m = r("negm", 64 * h, 64 * h + 64)
+            act(m, m, Fn.Identity, bias=tk(t, h))
 
     def masks(t, f):
         scatter(tab, r("lnr%d" % t, 0, 2), r("posc", P * t + 192, P * t + 224))
         f[0]()
         scatter(tab, r("land%d" % t, 0, 12), r("posc", P * t, P * t + 192))
         f[1]()
-        gather(r("lk", 0, 128), tab, r("nbu", 0, 8))
+        gather_add(r("lk", 0, 128), tab, r("nbu", 0, 8), r("bs", 0, 128))
         f[2]()
-        run_on(r("pv", 0, 128), r("lk", 0, 128), 128)
+        scan(r("pv", 0, 128), r("segm", 0, 128), r("lk", 0, 128), LOW, Op.add, Op.max)
         f[3]()
-        ts(r("zo", 0, 8), r("pv", 15, 128, st=16), cf(19), Op.subtract)
-        ts(r("zf", 0, 8), r("pv", 15, 128, st=16), cf(19), Op.subtract, -1.0, Op.add)
+        tt(r("zo", 0, 8), r("pv", 15, 128, st=16), b8, Op.subtract)
 
-    fill(r("ones", 0, 2), 1.0)
-    ts(r("negm", 0, 64), r("c16", 0, 64), cf(1), Op.not_equal, LOW, Op.mult)
-    settle(True)
+    dig = lambda y, h: r("oh", 512 + 8 * y + h, 512 + 8 * y + h + 7, st=6)
+    minus, two = r("k4", 0, 2), r("k4", 2, 4)
+    act(r("pz", 0, 2), place, bias=2048.0 * (P * rank + 1), scale=2048.0)
+    zeros("oh", 512, 40)
     for b in range(4):
         zeros("own", STR * b, OFF)
-    for d, b in enumerate((2, 21, 22, 23)):
-        act(r("plm", 64 * d, 64 * d + 64), r("ic", 64 * d, 64 * d + 64), Fn.Identity, bias=cf(b))
     for h in (0, 1):
-        act(r("ed", 512 * h + 1, 512 * h + 512, st=2), r("plm", 0, 256), Fn.Identity, bias=r("cf", 12 + h, 13 + h), scale=2.0 ** -120)
+        act(dig(2, h), two, scale=384.0)
+        act(dig(3, h), two, Fn.Identity, bias=2.0 * (OFF + 16 + 128 * h), scale=cf(2))
+        act(dig(4, h), two, Fn.Identity, bias=-32.0, scale=cf(0))
+    nop = lambda: None
 
-    def lows(h):
-        fill(r("zsb", ZW * h, ZW * h + 1), LOW)
-        fill(r("gs", 96 * h + 64, 96 * h + 96), LOW)
+    def seeds():
+        ts(r("tk", 0, 2), r("ofl", 15, 32, st=16), cf(5), Op.is_gt, LOW, Op.mult)
+        settle(0)
+        for h in (0, 1):
+            act(pk(0, h), r("pz", h, h + 1), Fn.Identity, scale=tk(0, h))
 
-    def digits(h):
-        ts(r("dg", 16 + h, 23 + h, st=6), r("ones", 0, 2), cf(2), Op.mult, float(OFF + 16 + 128 * h), Op.add)
-        ts(r("dg", 48 + 6 * h, 50 + 6 * h), r("ones", 0, 2), cf(0), Op.mult, -16.0, Op.add)
+    def lows():
+        ts(r("b8", 4, 8), r("b8", 4, 8), -1.0, Op.add)
+        fill(r("zsb", 0, 2), LOW)
 
-    digits(0)
-    digits(1)
-    masks(0, [lambda: lows(0), lambda: lows(1), lambda: quant("dpq", "dpqs", 0, 128, "dg", 0, 512),
-              lambda: ts(r("segm", 0, 64), r("c16", 0, 64), 0.0, Op.is_equal, LOW, Op.mult)])
+    run_on(r("ofl", 0, 32), r("olk", 0, 32), 32)
+    masks(0, [seeds, lambda: ts(r("segm", 0, 128), r("c16", 0, 128), 0.0, Op.is_equal, LOW, Op.mult), lows,
+              lambda: ts(r("thr", 0, 32), r("c32", 0, 32), cf(0), Op.is_lt, TINY, Op.mult)])
+    ts(r("cf", 6, 8), r("cf", 3, 5), 0.0, Op.is_gt, -TINY, Op.mult)
+    ts(r("cf", 8, 10), r("k2", 0, 2), cf(1), Op.add)
 
-    def move(e, out, a):
-        if e == "v":
-            cp(out, a)
-        else:
-            act(out, a, Fn.Copy)
+    def y_put(t, o):
+        scatter(r("sy", STR * o, STR * o + STR), r("pl", 2 * t, 2 * t + 2), r("yb", 64 * t + S * o, 64 * t + S * o + S))
 
     for t in range(R):
-        c = "comb%d" % t
+        c, a0 = fresh(t)
         more = t < R - 1
-        zs = lambda h, a, w: r("zsb", ZW * h + 1 + P * t + a, ZW * h + 1 + P * t + a + w)
-        keep = lambda b: act(r("par", PW * b + P * t, PW * b + P * t + P), r("dec", 512 * b, 512 * b + P), Fn.Copy)
+        pl = r("pl", 2 * t, 2 * t + 2)
+        zs = lambda h, a: r("zsb", 2 + 2 * (P * t + a) + h, 2 + 2 * (P * t + a + 128), st=2)
+        keep = lambda b: act(r("par", PW * b + P * t, PW * b + P * t + P), r("dec", 512 * b, 512 * b + P))
         for h in (0, 1):
-            mm("zz", 2 + h, 128, "qx", 128 * h, c, 192)
-            act(zs(h, 192, 64), r("zz", 1024 + 512 * h, 1088 + 512 * h), Fn.Copy)
+            mm("zz", h, 128, "big", 128 * h, c, a0 + 128)
+            act(zs(h, 128), r("zz", 512 * h, 512 * h + 128))
         for h in (0, 1):
-            mm("zz", h, 128, "qx", 128 * h, c, 0)
-            act(zs(h, 0, 128), r("zz", 512 * h, 512 * h + 128), Fn.Copy)
-        for h in (0, 1):
-            mm("zz", 2 + h, 128, "qx", 128 * h, c, 128)
-            act(zs(h, 128, 64), r("zz", 1024 + 512 * h, 1088 + 512 * h), Fn.Copy)
+            mm("zz", 2 + h, 128, "big", 128 * h, c, a0)
+        act(zs(0, 0), r("zz", 1024, 1152))
+        cp(zs(1, 0), r("zz", 1536, 1664))
         for b in range(4):
-            mm("dec", b, P, "eq", 128 * b, c, 0)
+            mm("dec", b, P, "eq", 128 * b, c, a0)
         keep(0)
 
-        def scores(h):
-            w, o, q = r("zsb", ZW * h, ZW * h + 1 + P * t + P), r("zo", 4 * h, 4 * h + 4), r("gs", 96 * h, 96 * h + 64)
-            op("v", lambda: g.vector.tensor_tensor(ap(q), ap(w).indirect(ap(o)), T.negm[:, 0:64], Op.add), [w, o, r("negm", 0, 64)], [q])
-
-        def own_scores(h):
-            scan(r("sbx", 64 * h, 64 * h + 64), r("segm", 0, 64), r("gs", 96 * h, 96 * h + 64), LOW, Op.add, Op.max)
-
-        def best(h):
-            a = r("gs", 96 * h, 96 * h + 96)
-            scan(r("sc", 96 * h, 96 * h + 96), a, a, LOW, Op.max, Op.max)
-
-        sb = lambda h: r("sbx", 15 + 64 * h, 64 + 64 * h, st=16)
-        bst = lambda h: r("sc", 96 * h + 95, 96 * h + 96)
-        k4 = lambda name, h: r(name, 4 * h, 4 * h + 4)
-        isbest = lambda h: ts(k4("e8", h), sb(h), bst(h), Op.is_equal)
-        turn = lambda h: tr(r("row", 32 * h, 32 * h + 32), r("sc", 96 * h + 64, 96 * h + 96))
-        scores(0)
-        scores(1)
-        best(0)
-        best(1)
-        turn(0)
-        own_scores(0)
-        turn(1)
-        own_scores(1)
+        gs = lambda h, st=1: r("gs", 64 * h, 64 * h + 64, st=st)
+        bst = lambda h: r("sc", 64 * h + 63, 64 * h + 64)
+        for h in (0, 1):
+            gather_add(gs(h), r("zsb", 0, 2 + 2 * P * (t + 1)), r("zo", 4 * h, 4 * h + 4), r("negm", 64 * h, 64 * h + 64))
+        for h in (0, 1):
+            scan(r("sc", 64 * h, 64 * h + 64), gs(h), gs(h, -1), LOW, Op.max, Op.max)
+        for h in (0, 1):
+            tr(r("row", h, 64, st=2), r("sc", 64 * h + 32, 64 * h + 64))
+            act(r("ne", 64 * h, 64 * h + 64), gs(h), Fn.Sign, bias=bst(h), scale=-1.0)
+        ts(r("pen", 0, 2), r("sc", 63, 128, st=64), 0.5 * LOW, Op.is_lt, 1024.0, Op.mult)
         for b in range(4):
-            move("v" if b < 2 else "s", r("row", 64, 128, 32 * b, 32 * b + 32), r("row", 0, 64, 32 * (b ^ 1), 32 * (b ^ 1) + 32))
-        isbest(0)
+            (cp if b < 2 else act)(r("row", 64, 128, 32 * b, 32 * b + 32), r("row", 0, 64, 32 * (b ^ 1), 32 * (b ^ 1) + 32))
+        scan(r("sl", 0, 128), r("ne", 0, 128), r("lk", 0, 128), 0.0, Op.mult, Op.max)
+        for h in (0, 1):
+            act(r("df", 32 * h, 32 * h + 32), r("row", h, 64, st=2), Fn.Identity, bias=bst(h), scale=-1.0)
         for b in (0, 1):
-            move("v" if b < 1 else "s", r("row", 128, 256, 64 * b, 64 * b + 64), r("row", 0, 128, 64 * (1 - b), 64 * (1 - b) + 64))
+            act(r("row", 128, 256, 64 * b, 64 * b + 64), r("row", 0, 128, 64 * (1 - b), 64 * (1 - b) + 64))
+        sel = r("sl", 63, 128, st=64)
+        act(r("a2", 2, 4), sel, bias=STEP2K)
+        act(r("b2", 2, 4), sel, bias=STEP64)
+        act(r("a2", 0, 2), r("a2", 2, 4), bias=-STEP2K)
+        act(r("b2", 0, 2), r("b2", 2, 4), bias=-STEP64)
+        for h in (0, 1):
+            act(dig(1, h), minus, Fn.Identity, bias=r("sl", 64 * h + 63, 64 * h + 64), scale=r("b2", h, h + 1))
+            act(dig(0, h), minus, Fn.Identity, bias=r("b2", h, h + 1), scale=r("a2", h, h + 1))
+        for b in (1, 2, 3):
+            keep(b)
 
-        def differ(e, h, i):
-            a, o = r("row", 128 * i, 128 * i + 128), r("ed", 512 * h + 256 * i, 512 * h + 256 * i + 256, st=2)
-            if e == "v":
-                ts(o, a, -1.0, Op.mult, bst(h), Op.add)
-            else:
-                act(o, a, Fn.Identity, bias=bst(h), scale=-1.0)
-
-        differ("v", 0, 0)
-        differ("s", 1, 0)
-        differ("s", 0, 1)
-        differ("s", 1, 1)
-        isbest(1)
-
-        def ahead(x, w):
-            scan(r("cm", x, x + w), r("ste", 0, w), r("ed", x, x + w), 0.0, Op.mult, Op.add)
-
-        def count(h):
-            act(r("sg", 256 * h, 256 * h + 256), r("cm", 512 * h + 1, 512 * h + 512, st=2), Fn.Sign, accum=r("rs", h, h + 1))
-
-        def slots(h):
-            ts(r("oh", h, 512, st=2), r("pat", 0, 256), r("rs", h, h + 1), Op.is_equal, r("val", h, h + 1), Op.mult)
-
-        ahead(0, 256)
-        ahead(256, 256)
-        count(0)
-        ahead(512, 256)
-        ahead(768, 256)
-        count(1)
-        ts(r("val", 0, 2), r("sc", 95, 192, st=96), -1e29, Op.is_gt)
-        tt(r("t8", 0, 8), r("e8", 0, 8), r("zf", 0, 8), Op.mult)
-        ts(r("ne8", 0, 8), r("e8", 0, 8), -1.0, Op.mult, 1.0, Op.add)
-        slots(0)
-        scan(r("sf", 0, 8), r("ne8", 0, 8), r("t8", 0, 8), 0.0, Op.mult, Op.add)
-        loc2 = r("sf", 3, 8, st=4)
-        top = 8 if t == 2 else 0
-        slots(1)
-        ts(r("hf", 0, 2), loc2, STEP32, Op.add, STEP32, Op.subtract)
-        quant("ohq", "ohqs", 0, 128, "oh", 0, 512)
-        mm("zz", 2, 128, "ohq", 0, "dpq", 0)
-        keep(1)
+        fl = lambda h, a, w: r("fl", 256 * h + a, 256 * h + a + w)
+        ahead = lambda h, a, w, row, th: ts(fl(h, a, w), row, bst(h), Op.subtract, th, Op.is_gt)
+        for h in (0, 1):
+            ahead(h, 32, 32, r("row", 64 + h, 128, st=2), cf(6))
+        for h in (0, 1):
+            tt(fl(h, 0, 32), r("df", 32 * h, 32 * h + 32), r("thr", 0, 32), Op.is_lt)
+        for h in (0, 1):
+            ahead(h, 64, 64, r("row", 1 - h, 128, st=2), -TINY * h)
+        for h in (0, 1):
+            ahead(h, 128, 64, r("row", 128 + h, 256, st=2), cf(7))
+            ahead(h, 192, 64, r("row", 129 - h, 256, st=2), -TINY * h)
+        for h in (0, 1):
+            scan(r("cn", 128 * h, 128 * h + 128), fl(h, 0, 128), fl(h, 128, 128), r("pen", h, h + 1), Op.add, Op.add)
+        for h in (0, 1):
+            ts(r("oh", h, 512, st=2), r("pat", 0, 256), r("cn", 128 * h + 127, 128 * h + 128), Op.is_equal, 0.5, Op.mult)
+        ts(r("tk", 2 * t + 2, 2 * t + 4), r("cn", 127, 256, st=128), S - 0.5, Op.is_lt, LOW, Op.mult)
+        quant("ohq", 0, 138, "oh", 0, 552)
+        mm("zz", 2, 128, "ohq", 0, "ohq", 10)
+        if t:
+            y_put(t - 1, 0)
+            y_put(t - 1, 1)
+        if more:
+            settle(t + 1)
+        for h in (0, 1):
+            act(pk(t + 1, h), r("a2", h, h + 1), Fn.Identity, bias=pk(t, h), scale=tk(t + 1, h))
+        out = lambda i: r("zz", 1142 + i, 1143 + i)
         for u in (0, 1):
-            act(r("dg", 6 * u, 6 * u + 2), r("hf", 0, 2), Fn.Copy, bias=-32.0 * top)
-            tt(r("dg", 32 + 6 * u, 34 + 6 * u), loc2, r("hf", 0, 2), Op.subtract)
-        keep(2)
-        quant("dgq", "dgqs", 0, 128, "dg", 0, 512)
-        mm("zz", 3, 128, "ohq", 0, "dgq", 0)
-        out = lambda i: r("zz", 1024 + i, 1025 + i)
-        for u, k in enumerate((1, 25)):
-            ts(r("pl", u, u + 1), out(4 + u), out(12 + u), Op.add, cf(k), Op.max)
-        keep(3)
-        ts(r("tk", 0, 1), r("rs", 0, 1), 193.0, Op.is_gt, r("val", 0, 1), Op.mult)
+            ts(r("pl", 2 * t + u, 2 * t + u + 1), out(6 + u), out(8 + u), Op.add, cf(8 + u), Op.max)
         my = "my%d" % (t + 1)
-        lv = P - 1 + S * t
-        located = lambda: scatter(r("loc", base - OFF, base + P), r("pl", 0, 2), r("posc", lv, lv + S))
-        if more:
-            ts(r(my, 0, 2), r("pl", 0, 2), float(STR * rank), Op.add)
-        else:
-            located()
+        located = lambda: scatter(r("loc", 0, STR), pl, r("lv", S * t, S * t + S))
         for b in range(4):
-            gather_s(r("od", 32 * b, 32 * b + 32), r("own", STR * b, STR * b + STR), r("pl", 0, 2))
+            gather_s(r("od", 32 * b, 32 * b + 32), r("own", STR * b, STR * b + STR), pl)
+        ts(r("offp", 0, 1), out(0), out(2), Op.add, out(4), Op.add)
         if more:
+            ts(r(my, 0, 2), pl, float(STR * rank), Op.add)
             send_list(t + 1)
-        for u in (0, 1):
-            ts(r("offp", u, u + 1), out(512 + u), out(520 + u), Op.add, 32.0 * top, Op.add)
-        ts(r("tk", 1, 2), r("rs", 1, 2), 193.0, Op.is_gt, r("val", 1, 2), Op.mult)
-
-        def numbers(i):
-            if i == 0:
-                if t == 0:
-                    ts(nb3, nbo, 1.0, Op.add)
-                    ts(r("z2", 0, 2), place2, float(P * rank + 1), Op.add)
-                    tt(r("w3", 0, 2), r("z2", 0, 2), r("tk0", 0, 2), Op.mult)
-                    ts(r("pa2", 0, 2), r("w3", 0, 2), -1.0, Op.add)
-                tt(r("u8", 0, 8), r("e8", 0, 8), nb3, Op.mult)
-            else:
-                scan(r("sn", 0, 8), r("ne8", 0, 8), r("u8", 0, 8), 0.0, Op.mult, Op.add)
-
-        def parents(i):
-            if i == 0:
-                tt(r("y2", 0, 2), r("sn", 3, 8, st=4), r("tk", 0, 2), Op.mult)
-            else:
-                tt(r("pa2", 0, 2), r("pa2", 0, 2), r("y2", 0, 2), Op.add)
-
-        half_row = lambda m: run_on(r("flx", 128 * m, 128 * m + 128), r("loc", base + 128 * m, base + 128 * m + 128), 128)
-        half_list = lambda m: ts(r("fo", 8 * m, 8 * m + 8), r("flx", 128 * m + 15, 128 * m + 128, st=16), cf(19), Op.subtract)
-
-        def blend(b):
-            w, o, a, q = r("par", PW * b, PW * b + P * t + P), r("offp", 0, 2), r("od", 32 * b, 32 * b + 32), r("ht", b, 128, st=4)
-            op("v", lambda: g.vector.tensor_tensor(ap(q), ap(w).indirect(ap(o)), ap(a), Op.add), [w, o, a], [q])
-
-        def y_of(cq, a):
-            for o in (0, 1):
-                mm("dec", o, 128, "qw", 128 * o, cq, a)
-                act(r("yb", S * o, S * o + S), r("dec", 512 * o, 512 * o + S), Fn.Copy)
-
-        y_put = lambda o: scatter(r("sy", STR * o, STR * o + STR), r("pl", 0, 2), r("yb", S * o, S * o + S))
+        ts(r("offp", 1, 2), out(1), out(3), Op.add, out(5), Op.add)
+        if not more:
+            located()
 
         for b in range(4):
-            blend(b)
-        if more:
-            d, o = "comb%d" % (t + 1), 224
-            quant(d, d + "s", o, o + 128, "ht", 0, 512)
-            send_cols(t + 1)
-            dmas("df%d" % t, copies(d, o, "finw", P + S * t, S))
-            if t == 0:
-                quant("qw", "qws", 0, 256, "wt", 0, 1024)
-                for u in (0, 1):
-                    mm("zz", u, 256, "qw", 128 * u, "qx", 0)
-                    act(r("sy", STR * u + OFF, STR * u + STR), r("zz", 512 * u, 512 * u + 256), Fn.Copy)
-            numbers(0)
-            y_of(d, o)
-            scatter(tab, r(my, 0, 2), r("posc", P * (t + 1) + 224, P * (t + 1) + 256))
-            settle(False)
-            masks(t + 1, [located, lambda: numbers(1), lambda: parents(0), lambda: parents(1)])
-            y_put(0)
-            y_put(1)
-        else:
-            half_row(0)
-            quant("finw", "finws", 320, 448, "ht", 0, 512)
-            y_of("finw", 320)
-            half_row(1)
-            half_list(0)
-            numbers(0)
-            half_list(1)
-            numbers(1)
-            pick("fin", 0, "finw", 352, "fo", 0, 16)
-            y_put(0)
-            y_put(1)
-            parents(0)
-            parents(1)
+            gather_add(r("xt", b, HT, st=4), r("par", PW * b, PW * b + P * t + P), r("offp", 0, 2), r("od", 32 * b, 32 * b + 32))
+        o = P + CW * t + 7 * S
 
-    dmas("dout", [("y", T.oc[:], T.fin[:].bitcast(dt.uint8), [r("fin", 0, 256)], [])] +
-         [("s", T.osc[4 * k:4 * k + 4, :], T.fins[32 * k:32 * k + 4, :], [r("fins", 0, 256)], []) for k in range(4)] +
-         [("y", T.y[:, 256 * o:256 * o + 256], T.sy[:, STR * o + OFF:STR * o + STR], [r("sy", STR * o, STR * o + STR)], []) for o in (0, 1)])
-    dmas("dpa", [("s", T.pa[0:1, 128 * h:128 * h + 128], T.pa2[:, h:h + 1], [r("pa2", h, h + 1)], []) for h in (0, 1)])
+        def y_of():
+            for u in (0, 1):
+                mm("dec", u, 128, "qw", 128 * u, "big", o)
+                act(r("yb", 64 * t + S * u, 64 * t + S * u + S), r("dec", 512 * u, 512 * u + S))
+
+        if more:
+            quant("big", o, o + 128, "xt", 0, 512)
+            send_cols(t + 1, nop)
+            scatter(tab, r(my, 0, 2), r("posc", P * (t + 1) + 224, P * (t + 1) + 256))
+            if t == 0:
+                quant("qw", 0, 256, "wt", 0, 1024)
+                for u in (0, 1):
+                    mm("zz", u, 256, "qw", 128 * u, "big", 0)
+                    act(r("sy", STR * u + OFF, STR * u + STR), r("zz", 512 * u, 512 * u + 256))
+            y_of()
+            masks(t + 1, [located, nop, nop, nop])
+        else:
+            pz = lambda i: r("pz", 2 * i, 2 * i + 2)
+            act(pz(0), r("pk", 6, 8), bias=-1024.5, scale=1.0 / (2048.0 * LOW))
+            act(pz(1), r("pk", 6, 8), bias=-1.0, scale=1.0 / (2048.0 * LOW))
+            act(pz(2), pz(0), bias=STEP2K)
+            act(pz(3), pz(2), Fn.Relu, bias=-STEP2K)
+            for h in (0, 1):
+                act(r("pa2", h, h + 1), r("pz", 6 + h, 7 + h), Fn.Identity, bias=r("pz", 2 + h, 3 + h), scale=-1.0)
+            dmas("dpa", [("y", T.pa[0:1, 128 * h:128 * h + 128], T.pa2[:, h:h + 1], [r("pa2", h, h + 1)], []) for h in (0, 1)])
+            half_row = lambda m: run_on(r("flx", 128 * m, 128 * m + 128), r("loc", OFF + 128 * m, OFF + 128 * m + 128), 128)
+            half_list = lambda m: ts(r("fo", 8 * m, 8 * m + 8), r("flx", 128 * m + 15, 128 * m + 128, st=16), cf(5), Op.subtract)
+            half_row(0)
+            quant("big", o, o + 128, "xt", 0, 512)
+            y_of()
+            half_list(0)
+            half_row(1)
+            pick("fin", 0, "big", o + S, "fo", 0, 8)
+            half_list(1)
+            y_put(t, 0)
+            y_put(t, 1)
+            pick("fin", 128, "big", o + S, "fo", 8, 16)
+
+    oc = lambda m: ("y", T.oc[:, 512 * m:512 * m + 512], T.fin[:, 128 * m:128 * m + 128].bitcast(dt.uint8), [r("fin", 128 * m, 128 * m + 128)], [])
+    dmas("dout", [oc(0)] +
+         [("y", T.y[:, 256 * o:256 * o + 256], T.sy[:, STR * o + OFF:STR * o + STR], [r("sy", STR * o, STR * o + STR)], []) for o in (0, 1)] +
+         [oc(1)] + [("s", T.osc[4 * k:4 * k + 4, :], T.fins[32 * k:32 * k + 4, :], [r("fins", 0, 256)], []) for k in range(4)])
     for sem in cnt:
         if known["g"].get(sem, 0) < cnt[sem]:
             g.wait_ge(T.sem[sem], cnt[sem])

import numpy as np
from concourse.bass import DstId, RemoteDMATransfer
from concourse.mybir import dt, AluOpType as Op, AxisListType, ActivationFunctionType as Fn

F8 = "float8_e4m3fn_x4"
CW = 384
STR, OFF = 304, 48
TAB = 8 * STR
PW = 768
HT = 128
STEP64, STEP2K = 1.5 * 2.0 ** 29, 1.5 * 2.0 ** 34
LOW, TINY = -2.0 ** 99, 2.0 ** -100
SCRATCH = {"dec": ("psum", [128, 2048], "float32"), "zz": ("psum", [128, 2048], "float32")}
for _n, _w in (("big", 256 + 3 * CW), ("qw", 256), ("eq", 512), ("comb0", 256), ("fin", 256), ("ohq", 138)):
    SCRATCH[_n] = ("sbuf", [128, _w], F8)
    SCRATCH[_n + "s"] = ("sbuf", [128, _w], "uint8")
for _d, _l in (("bfloat16", (("xt", HT + 1024), ("wt", 1024), ("half", 256), ("et", 528), ("par", 4 * PW), ("own", 4 * STR), ("fl", 512),
                             ("cn", 256), ("pat", 256), ("oh", 552))),
               ("int32", (("sdw", 2), ("nbw", 64), ("nbi", 8), ("nbsh", 8), ("pint", 1), ("ci", 8))),
               ("uint16", (("sdu", 2), ("nbu", 8), ("rep", 8), ("oix", 2), ("my0", 2), ("my1", 2), ("my2", 2), ("land0", 16), ("land1", 16),
                           ("land2", 16), ("lnr0", 2), ("lnr1", 2), ("lnr2", 2), ("zo", 8), ("pl", 6), ("offp", 2), ("fo", 16))),
               ("float32", (("yb", 192), ("od", 128), ("nba", 8), ("nbt", 8), ("b8", 8), ("pr", 8), ("olk", 32), ("ofl", 32), ("place", 2),
                            ("c16", 128), ("c32", 32), ("k4", 4), ("k2", 2), ("cf", 16), ("posc", 768), ("lv", 96), ("tab", TAB), ("loc", STR),
                            ("hm", 128), ("negm", 128), ("segm", 128), ("bs", 128), ("lk", 128), ("pv", 128), ("zsb", 2 + 2 * PW),
                            ("gs", 128), ("sc", 128), ("ne", 128), ("sl", 128), ("row", 256), ("df", 64), ("thr", 32), ("pen", 2),
                            ("a2", 4), ("b2", 4), ("tk", 8), ("pk", 8), ("pz", 8), ("pa2", 2), ("flx", 256), ("sy", 2 * STR)))):
    for _n, _w in _l:
        SCRATCH[_n] = ("sbuf", [128, _w], _d)
SEMAPHORES = ["v", "s", "p", "gp", "dsd", "dx", "dnb", "dw", "dout", "dpa", "sent"] + ["ar%s%d" % (_x, _t) for _x in "lmsfcdn" for _t in range(3)]


def r(name, c0, c1, p0=0, p1=128, st=1):
    return (name, c0, c1, p0, p1, st)


def meet(a, b):
    if a[0] != b[0] or a[1] >= b[2] or b[1] >= a[2] or a[3] >= b[4] or b[3] >= a[4]:
        return False
    return not (a[5] == b[5] and a[5] > 1 and (a[1] - b[1]) % a[5])


def inside(a, b):
    return a[1] >= b[1] and a[2] <= b[2] and a[3] >= b[3] and a[4] <= b[4] and b[5] == 1


def rank_program(g, core, T, topo):
    rank = T.rank_of(core)
    if rank is None:
        return
    cores = list(T.cores)
    n = len(cores)
    S, P, R = 32, 256, 3

    eng = {"v": g.vector, "s": g.scalar, "p": g.tensor, "y": g.sync, "g": g}
    own = {"v": "v", "s": "s", "p": "p", "g": "gp"}
    known = {e: {} for e in eng}
    cnt = {}
    hist = {}
    seq = [0]

    def need(e, toks):
        for sem, val, clock, q in sorted(toks, key=lambda t: -t[3]):
            if known[e].get(sem, 0) < val:
                eng[e].wait_ge(T.sem[sem], val)
                known[e][sem] = val
                for k, c in clock.items():
                    known[e][k] = max(known[e].get(k, 0), c)

    def before(e, reads, writes):
        toks = []
        for a in reads:
            for b, kind, tok, f in hist.get(a[0], []):
                if kind == "w" and meet(a, b):
                    toks.append(tok)
        for a in writes:
            for b, kind, tok, f in hist.get(a[0], []):
                if meet(a, b):
                    toks.append(tok)
        need(e, toks)

    def note(e, reads, writes, tok):
        for a in writes:
            hist[a[0]] = [h for h in hist.get(a[0], []) if not inside(h[0], a)] + [(a, "w", tok, e)]
        for a in reads:
            hist[a[0]] = [h for h in hist.get(a[0], []) if not (h[1] == "r" and h[3] == e and inside(h[0], a))] + [(a, "r", tok, e)]

    def token(sem, clock):
        seq[0] += 1
        return (sem, cnt[sem], dict(clock), seq[0])

    def op(e, fn, reads, writes):
        before(e, reads, writes)
        sem = own[e]
        cnt[sem] = cnt.get(sem, 0) + 1
        fn().then_inc(T.sem[sem], 1)
        note(e, reads, writes, token(sem, known[e]))

    def dmas(sem, lst):
        for e, out, in_, reads, writes in lst:
            before(e, reads, writes)
            cnt[sem] = cnt.get(sem, 0) + 16
            eng[e].dma_start(out, in_).then_inc(T.sem[sem], 16)
        for e, out, in_, reads, writes in lst:
            note(sem, reads, writes, token(sem, {}))

    def ap(q):
        name, c0, c1, p0, p1, st = q
        if st < 0:
            return T[name][p0:p1, c1 - 1:(c0 - 1 if c0 else None):st]
        return T[name][p0:p1, c0:c1] if st == 1 else T[name][p0:p1, c0:c1:st]

    def tup(*xs):
        return [x for x in xs if isinstance(x, tuple)]

    def sv(x):
        return ap(x) if isinstance(x, tuple) else x

    def ts(out, a, s1, op0, s2=None, op1=None):
        if op1 is None:
            op("v", lambda: g.vector.tensor_scalar(ap(out), ap(a), sv(s1), None, op0), [a] + tup(s1), [out])
        else:
            op("v", lambda: g.vector.tensor_scalar(ap(out), ap(a), sv(s1), sv(s2), op0, op1), [a] + tup(s1, s2), [out])

    def tt(out, a, b, o):
        op("v", lambda: g.vector.tensor_tensor(ap(out), ap(a), ap(b), o), [a, b], [out])

    def cp(out, a):
        op("v", lambda: g.vector.tensor_copy(ap(out), ap(a)), [a], [out])

    def tr(out, a):
        op("v", lambda: g.vector.transpose(ap(out), ap(a)), [a], [out])

    def scan(out, a, b, init, o0, o1):
        op("v", lambda: g.vector.tensor_tensor_scan(ap(out), ap(a), ap(b), sv(init), o0, o1), [a, b] + tup(init), [out])

    def fill(out, c):
        op("v", lambda: g.vector.memset(ap(out), c), [], [out])

    def iota(out, pattern, base, cm, flag=True):
        if flag:
            op("g", lambda: g.iota(ap(out), pattern, base, cm, allow_small_or_imprecise_dtypes=True), [], [out])
        else:
            op("g", lambda: g.iota(ap(out), pattern, base, cm), [], [out])

    def act(out, a, func=Fn.Copy, bias=0.0, scale=1.0):
        op("s", lambda: g.scalar.activation(ap(out), ap(a), func, bias=sv(bias), scale=sv(scale)), [a] + tup(bias, scale), [out])

    def quant(c, a, b, src, x0, x1):
        s = c + "s"
        op("v", lambda: g.vector.quantize_mx(T[c][:, a:b], T[s][:, a:b], T[src][:, x0:x1]), [r(src, x0, x1)], [r(c, a, b), r(s, a, b)])

    def gather(out, win, off):
        op("v", lambda: g.vector.tensor_copy(ap(out), ap(win).indirect(ap(off))), [win, off], [out])

    def gather_add(out, win, off, b):
        op("v", lambda: g.vector.tensor_tensor(ap(out), ap(win).indirect(ap(off)), ap(b), Op.add), [win, off, b], [out])

    def gather_s(out, win, off):
        op("s", lambda: g.scalar.activation(ap(out), ap(win).indirect(ap(off)), Fn.Copy), [win, off], [out])

    def scatter(win, off, a):
        op("v", lambda: g.vector.tensor_copy(ap(win).indirect(ap(off)), ap(a)), [a, off], [win])

    def pick(c2, a2, c1, w, off, o0, o1):
        k = 16 * (o1 - o0)
        s2, s1 = c2 + "s", c1 + "s"
        op("v", lambda: g.vector.tensor_copy(T[c2][:, a2:a2 + k].bitcast(dt.uint32), T[c1][:, 0:w].bitcast(dt.uint32).indirect(T[off][:, o0:o1])),
           [r(c1, 0, w), r(off, o0, o1)], [r(c2, a2, a2 + k)])
        op("s", lambda: g.scalar.activation(T[s2][:, a2:a2 + k], T[s1][:, 0:w].indirect(T[off][:, o0:o1]), Fn.Copy),
           [r(s1, 0, w), r(off, o0, o1)], [r(s2, a2, a2 + k)])

    def mm(out, bank, width, c1, a1, c2, a2):
        op("p", lambda: g.tensor.matmul_mx(T[out][:, 512 * bank:512 * bank + width], T[c1][:, a1:a1 + 128], T[c1 + "s"][:, a1:a1 + 128],
                                           T[c2][:, a2:a2 + width], T[c2 + "s"][:, a2:a2 + width], True, True),
           [r(c1, a1, a1 + 128), r(c1 + "s", a1, a1 + 128), r(c2, a2, a2 + width), r(c2 + "s", a2, a2 + width)],
           [r(out, 512 * bank, 512 * bank + 512)])

    mate = rank ^ 1
    assert topo.chip(cores[mate]) == topo.chip(core)
    far = [q for q in range(n) if topo.chip(cores[q]) != topo.chip(core)]
    level = sorted((q for q in far if topo.die(cores[q]) == topo.die(core)), key=lambda q: q ^ rank)
    cross = [q ^ 1 for q in level]
    block = (cross[::-1] + level[::-1] + [mate, rank]).index
    fe = topo.engines(core, cores[far[0]])
    ne = [e for e in topo.engines(core, cores[mate]) if e not in fe]
    fresh = lambda t: ("comb0", 0) if t == 0 else ("big", P + CW * (t - 1))

    def send(reads, parts):
        before("g", reads, [])
        out = []
        for es, sem, src, to in parts:
            ids = [topo.addr(cores[q]) for q, d in to]
            out.append(RemoteDMATransfer(dst_ids=[DstId(rid=a[0], pnc=a[1]) for a in ids], dma_engine_mask=sum(1 << e for e in es),
                                         remote_sem=T.sem[sem], srcs=[src], dsts=[d for q, d in to], alu_op=0))
            cnt["sent"] = cnt.get("sent", 0) + len(es)
        g.remote_dma_fused(out, local_sem=T.sem["sent"])

    def landed(sem, total, regions):
        cnt[sem] = total
        seq[0] += 1
        for a in regions:
            note("far", [], [a], (sem, total, {}, seq[0]))

    def send_list(t):
        src, to = T["my%d" % t][:, 0:2], lambda q: (q, T["land%d" % t][:, 2 * block(q):2 * block(q) + 2])
        send([r("my%d" % t, 0, 2)], [(fe, "arl%d" % t, src, [to(q) for q in far]), (ne, "arm%d" % t, src, [(mate, T["lnr%d" % t][:, 0:2])])])
        landed("arm%d" % t, len(ne), [r("lnr%d" % t, 0, 2)])
        landed("arl%d" % t, len(fe) * len(far), [r("land%d" % t, 0, 12)])

    def send_cols(t, meanwhile):
        c, a = fresh(t)
        s = c + "s"
        sc = lambda i, k=1: T[s][:, a + S * i:a + S * (i + k)]
        co = lambda i: T[c][:, a + S * i:a + S * i + S].bitcast(dt.uint8)
        at = lambda name, i, k=1: r(name, a + S * i, a + S * (i + k))
        ars, arf, arc, ard, arn = ["ar%s%d" % (x, t) for x in "sfcdn"]
        send([at(s, 7)], [(fe, ars, sc(7), [(q, sc(block(q))) for q in level]), (ne, arn, sc(7), [(mate, sc(6))])])
        send([at(c, 7)], [(fe, arf, co(7), [(level[0], co(5))]), (ne, arn, co(7), [(mate, co(6))])])
        send([at(c, 7)], [(fe, arc, co(7), [(level[1], co(4))])])
        rest = level[2:] + cross[1:]
        send([at(c, 7)], [(fe, ard, co(7), [(q, co(block(q))) for q in rest])])
        landed(arn, 2 * len(ne), [at(c, 6), at(s, 6)])
        landed(ars, 3 * len(fe), [at(s, 3, 3)])
        landed(arf, len(fe), [at(c, 5)])
        landed(arc, len(fe), [at(c, 4)])
        meanwhile()
        send([at(s, 3, 3)], [(ne, ard, sc(3, 3), [(mate, sc(0, 3))])])
        send([at(c, 5)], [(ne, ard, co(5), [(mate, co(2))])])
        landed(ard, len(fe) * len(rest) + 2 * len(ne), [at(c, 0, 4), at(s, 0, 3)])

    dmas("dsd", [(q, T.sdw[16 * a:16 * a + 16, :], T.sd[:], [], [r("sdw", 0, 2, 16 * a, 16 * a + 16)]) for a, q in enumerate("ysys")])
    dmas("dx", [("y", T.xt[:, HT:], T.x[:], [], [r("xt", HT, HT + 1024)])])
    dmas("dnb", [("y", T.nbw[16 * a:16 * a + 16, 0:57], T.nb[:, a:a + 57], [], [r("nbw", 0, 57, 16 * a, 16 * a + 16)]) for a in range(8)])
    dmas("dw", [("y", T.wt[:], T.w[:], [], [r("wt", 0, 1024)])])

    base = STR * rank + OFF
    pint, place = r("pint", 0, 1), r("place", 0, 2)
    iota(pint, [[0, 1]], 0, 1, False)
    iota(place, [[128, 2]], 0, 1)
    ci = lambda i: r("ci", i, i + 1)
    cf = lambda i: r("cf", i, i + 1)
    fill(r("half", 0, 256), 0.5)
    fill(r("et", 0, 528), 0.0)

    def zeros(name, a, w):
        act(r(name, a, a + w), r("half", 0, w), scale=0.0)

    for b in range(9):
        zeros("tab", 256 * b, 256)
    e_, h_ = r("et", 3, 515, st=4), r("half", 0, 128)
    op("g", lambda: g.affine_select(ap(e_), ap(h_), [[-1, 128]], Op.is_equal, 0.0, 0, 1), [h_], [e_])
    iota(r("c16", 0, 128), [[0, 8], [1, 16]], 0, 0)
    for i, m in enumerate((31, 15, 96, 32, 64)):
        ts(ci(i), pint, m, Op.bitwise_and)
    ts(r("oix", 0, 2), place, float(base), Op.add)
    cp(r("cf", 0, 5), r("ci", 0, 5))

    for b in range(2):
        ts(r("my0", 0, 2, 64 * b, 64 * b + 64), r("sdw", 0, 2, 0, 64), float(base), Op.add)
    send_list(0)
    iota(r("posc", 0, 256), [[2, 256]], 2, 0)
    iota(r("pr", 0, 8), [[0, 2], [-1, 4]], 3, 0)
    for b in range(2):
        cp(r("sdu", 0, 2, 64 * b, 64 * b + 64), r("sdw", 0, 2, 0, 64))
    unpacker = lambda b: quant("eq", 128 * b, 128 * b + 128, "et", 3 - b, 515 - b)
    for b in range(3):
        unpacker(b)
    quant("big", 0, 256, "xt", HT, HT + 1024)
    ts(cf(5), cf(1), -2048.0, Op.mult, 30720.0, Op.add)
    pick("comb0", 7 * S, "big", 256, "sdu", 0, 2)

    def small():
        iota(r("k4", 0, 4), [[3, 2], [0, 2]], -1, 0)
        iota(r("c32", 0, 32), [[1, 32]], 0, 0)

    send_cols(0, small)
    unpacker(3)
    zeros("tab", 256 * 9, TAB - 256 * 9)
    iota(r("k2", 0, 2), [[16, 2]], 1, 0)
    iota(r("pat", 0, 256), [[0, 8], [1, 16], [16, 2]], 0, 0)
    iota(r("posc", 256, 768), [[2, 512]], 514, 0)
    iota(r("loc", OFF, STR), [[1, P]], 0, 0)
    iota(r("lv", 0, 96), [[CW, 3], [1, S]], P + 7 * S, 0)

    tab, negm = r("tab", 0, TAB), r("negm", 0, 128)
    nbi, b8 = r("nbi", 0, 8), r("b8", 0, 8)
    for k in range(4):
        cp(r("nbi", 3 - k, 8, st=4), r("nbw", 16 * k, 16 * k + 9, st=8))
    ts(negm, r("c16", 0, 128), cf(1), Op.not_equal, LOW, Op.mult)
    act(r("pr", 0, 8), r("pr", 0, 8), scale=2.0 ** 22)
    act(r("hm", 0, 128), negm, bias=-131072.0, scale=133120.0 / LOW)
    for b in range(4):
        mm("dec", b, 256, "eq", 128 * b, "big", 0)
        act(r("own", STR * b + OFF, STR * b + STR), r("dec", 512 * b, 512 * b + 256))
    ts(r("nbt", 0, 8), nbi, 2048.0, Op.mult, 2048.0 - 770.0, Op.add)
    ts(r("nbsh", 0, 8), nbi, 8, Op.arith_shift_right)
    scatter(tab, r("my0", 0, 2), r("posc", 224, 256))
    cp(r("rep", 0, 8), r("c16", 0, 8))
    tt(b8, r("nbt", 0, 8), r("pr", 0, 8), Op.add)
    ts(r("nba", 0, 8), r("nbsh", 0, 8), float(STR - P), Op.mult, float(OFF), Op.add)
    gather(r("olk", 0, 32), tab, r("oix", 0, 2))
    gather_add(r("bs", 0, 128), b8, r("rep", 0, 8), negm)
    tt(r("nbu", 0, 8), r("nba", 0, 8), nbi, Op.add)

    def run_on(out, a, width):
        scan(out, r("hm", 0, width), a, 0.0, Op.add, Op.max)

    tk = lambda t, h: r("tk", 2 * t + h, 2 * t + h + 1)
    pk = lambda t, h: r("pk", 2 * t + h, 2 * t + h + 1)

    def settle(t):
        for h in (0, 1):
            m = r("negm", 64 * h, 64 * h + 64)
            act(m, m, Fn.Identity, bias=tk(t, h))

    def masks(t, f):
        scatter(tab, r("lnr%d" % t, 0, 2), r("posc", P * t + 192, P * t + 224))
        f[0]()
        scatter(tab, r("land%d" % t, 0, 12), r("posc", P * t, P * t + 192))
        f[1]()
        gather_add(r("lk", 0, 128), tab, r("nbu", 0, 8), r("bs", 0, 128))
        f[2]()
        scan(r("pv", 0, 128), r("segm", 0, 128), r("lk", 0, 128), LOW, Op.add, Op.max)
        f[3]()
        tt(r("zo", 0, 8), r("pv", 15, 128, st=16), b8, Op.subtract)

    dig = lambda y, h: r("oh", 512 + 8 * y + h, 512 + 8 * y + h + 7, st=6)
    minus, two = r("k4", 0, 2), r("k4", 2, 4)
    act(r("pz", 0, 2), place, bias=2048.0 * (P * rank + 1), scale=2048.0)
    zeros("oh", 512, 40)
    for b in range(4):
        zeros("own", STR * b, OFF)
    for h in (0, 1):
        act(dig(2, h), two, scale=384.0)
        act(dig(3, h), two, Fn.Identity, bias=2.0 * (OFF + 16 + 128 * h), scale=cf(2))
        act(dig(4, h), two, Fn.Identity, bias=-32.0, scale=cf(0))
    nop = lambda: None

    def seeds():
        ts(r("tk", 0, 2), r("ofl", 15, 32, st=16), cf(5), Op.is_gt, LOW, Op.mult)
        settle(0)
        for h in (0, 1):
            act(pk(0, h), r("pz", h, h + 1), Fn.Identity, scale=tk(0, h))

    def lows():
        ts(r("b8", 4, 8), r("b8", 4, 8), -1.0, Op.add)
        fill(r("zsb", 0, 2), LOW)

    run_on(r("ofl", 0, 32), r("olk", 0, 32), 32)
    masks(0, [seeds, lambda: ts(r("segm", 0, 128), r("c16", 0, 128), 0.0, Op.is_equal, LOW, Op.mult), lows,
              lambda: ts(r("thr", 0, 32), r("c32", 0, 32), cf(0), Op.is_lt, TINY, Op.mult)])
    ts(r("cf", 6, 8), r("cf", 3, 5), 0.0, Op.is_gt, -TINY, Op.mult)
    ts(r("cf", 8, 10), r("k2", 0, 2), cf(1), Op.add)

    def y_put(t, o):
        scatter(r("sy", STR * o, STR * o + STR), r("pl", 2 * t, 2 * t + 2), r("yb", 64 * t + S * o, 64 * t + S * o + S))

    for t in range(R):
        c, a0 = fresh(t)
        more = t < R - 1
        pl = r("pl", 2 * t, 2 * t + 2)
        zs = lambda h, a: r("zsb", 2 + 2 * (P * t + a) + h, 2 + 2 * (P * t + a + 128), st=2)
        keep = lambda b: act(r("par", PW * b + P * t, PW * b + P * t + P), r("dec", 512 * b, 512 * b + P))
        for h in (0, 1):
            mm("zz", h, 128, "big", 128 * h, c, a0 + 128)
            act(zs(h, 128), r("zz", 512 * h, 512 * h + 128))
        for h in (0, 1):
            mm("zz", 2 + h, 128, "big", 128 * h, c, a0)
        act(zs(0, 0), r("zz", 1024, 1152))
        cp(zs(1, 0), r("zz", 1536, 1664))
        for b in range(4):
            mm("dec", b, P, "eq", 128 * b, c, a0)
        keep(0)

        gs = lambda h, st=1: r("gs", 64 * h, 64 * h + 64, st=st)
        bst = lambda h: r("sc", 64 * h + 63, 64 * h + 64)
        for h in (0, 1):
            gather_add(gs(h), r("zsb", 0, 2 + 2 * P * (t + 1)), r("zo", 4 * h, 4 * h + 4), r("negm", 64 * h, 64 * h + 64))
        for h in (0, 1):
            scan(r("sc", 64 * h, 64 * h + 64), gs(h), gs(h, -1), LOW, Op.max, Op.max)
        for h in (0, 1):
            tr(r("row", h, 64, st=2), r("sc", 64 * h + 32, 64 * h + 64))
            act(r("ne", 64 * h, 64 * h + 64), gs(h), Fn.Sign, bias=bst(h), scale=-1.0)
        ts(r("pen", 0, 2), r("sc", 63, 128, st=64), 0.5 * LOW, Op.is_lt, 1024.0, Op.mult)
        for b in range(4):
            (cp if b < 2 else act)(r("row", 64, 128, 32 * b, 32 * b + 32), r("row", 0, 64, 32 * (b ^ 1), 32 * (b ^ 1) + 32))
        scan(r("sl", 0, 128), r("ne", 0, 128), r("lk", 0, 128), 0.0, Op.mult, Op.max)
        for h in (0, 1):
            act(r("df", 32 * h, 32 * h + 32), r("row", h, 64, st=2), Fn.Identity, bias=bst(h), scale=-1.0)
        for b in (0, 1):
            act(r("row", 128, 256, 64 * b, 64 * b + 64), r("row", 0, 128, 64 * (1 - b), 64 * (1 - b) + 64))
        sel = r("sl", 63, 128, st=64)
        act(r("a2", 2, 4), sel, bias=STEP2K)
        act(r("b2", 2, 4), sel, bias=STEP64)
        act(r("a2", 0, 2), r("a2", 2, 4), bias=-STEP2K)
        act(r("b2", 0, 2), r("b2", 2, 4), bias=-STEP64)
        for h in (0, 1):
            act(dig(1, h), minus, Fn.Identity, bias=r("sl", 64 * h + 63, 64 * h + 64), scale=r("b2", h, h + 1))
            act(dig(0, h), minus, Fn.Identity, bias=r("b2", h, h + 1), scale=r("a2", h, h + 1))
        for b in (1, 2, 3):
            keep(b)

        fl = lambda h, a, w: r("fl", 256 * h + a, 256 * h + a + w)
        ahead = lambda h, a, w, row, th: ts(fl(h, a, w), row, bst(h), Op.subtract, th, Op.is_gt)
        for h in (0, 1):
            ahead(h, 32, 32, r("row", 64 + h, 128, st=2), cf(6))
        for h in (0, 1):
            tt(fl(h, 0, 32), r("df", 32 * h, 32 * h + 32), r("thr", 0, 32), Op.is_lt)
        for h in (0, 1):
            ahead(h, 64, 64, r("row", 1 - h, 128, st=2), -TINY * h)
        for h in (0, 1):
            ahead(h, 128, 64, r("row", 128 + h, 256, st=2), cf(7))
            ahead(h, 192, 64, r("row", 129 - h, 256, st=2), -TINY * h)
        for h in (0, 1):
            scan(r("cn", 128 * h, 128 * h + 128), fl(h, 0, 128), fl(h, 128, 128), r("pen", h, h + 1), Op.add, Op.add)
        for h in (0, 1):
            ts(r("oh", h, 512, st=2), r("pat", 0, 256), r("cn", 128 * h + 127, 128 * h + 128), Op.is_equal, 0.5, Op.mult)
        ts(r("tk", 2 * t + 2, 2 * t + 4), r("cn", 127, 256, st=128), S - 0.5, Op.is_lt, LOW, Op.mult)
        quant("ohq", 0, 138, "oh", 0, 552)
        mm("zz", 2, 128, "ohq", 0, "ohq", 10)
        if t:
            y_put(t - 1, 0)
            y_put(t - 1, 1)
        if more:
            settle(t + 1)
        for h in (0, 1):
            act(pk(t + 1, h), r("a2", h, h + 1), Fn.Identity, bias=pk(t, h), scale=tk(t + 1, h))
        out = lambda i: r("zz", 1142 + i, 1143 + i)
        for u in (0, 1):
            ts(r("pl", 2 * t + u, 2 * t + u + 1), out(6 + u), out(8 + u), Op.add, cf(8 + u), Op.max)
        my = "my%d" % (t + 1)
        located = lambda: scatter(r("loc", 0, STR), pl, r("lv", S * t, S * t + S))
        for b in range(4):
            gather_s(r("od", 32 * b, 32 * b + 32), r("own", STR * b, STR * b + STR), pl)
        ts(r("offp", 0, 1), out(0), out(2), Op.add, out(4), Op.add)
        if more:
            ts(r(my, 0, 2), pl, float(STR * rank), Op.add)
            send_list(t + 1)
        ts(r("offp", 1, 2), out(1), out(3), Op.add, out(5), Op.add)
        if not more:
            located()

        for b in range(4):
            gather_add(r("xt", b, HT, st=4), r("par", PW * b, PW * b + P * t + P), r("offp", 0, 2), r("od", 32 * b, 32 * b + 32))
        o = P + CW * t + 7 * S

        def y_of():
            for u in (0, 1):
                mm("dec", u, 128, "qw", 128 * u, "big", o)
                act(r("yb", 64 * t + S * u, 64 * t + S * u + S), r("dec", 512 * u, 512 * u + S))

        if more:
            quant("big", o, o + 128, "xt", 0, 512)
            send_cols(t + 1, nop)
            scatter(tab, r(my, 0, 2), r("posc", P * (t + 1) + 224, P * (t + 1) + 256))
            if t == 0:
                quant("qw", 0, 256, "wt", 0, 1024)
                for u in (0, 1):
                    mm("zz", u, 256, "qw", 128 * u, "big", 0)
                    act(r("sy", STR * u + OFF, STR * u + STR), r("zz", 512 * u, 512 * u + 256))
            y_of()
            masks(t + 1, [located, nop, nop, nop])
        else:
            pz = lambda i: r("pz", 2 * i, 2 * i + 2)
            act(pz(0), r("pk", 6, 8), bias=-1024.5, scale=1.0 / (2048.0 * LOW))
            act(pz(1), r("pk", 6, 8), bias=-1.0, scale=1.0 / (2048.0 * LOW))
            act(pz(2), pz(0), bias=STEP2K)
            act(pz(3), pz(2), Fn.Relu, bias=-STEP2K)
            for h in (0, 1):
                act(r("pa2", h, h + 1), r("pz", 6 + h, 7 + h), Fn.Identity, bias=r("pz", 2 + h, 3 + h), scale=-1.0)
            dmas("dpa", [("y", T.pa[0:1, 128 * h:128 * h + 128], T.pa2[:, h:h + 1], [r("pa2", h, h + 1)], []) for h in (0, 1)])
            half_row = lambda m: run_on(r("flx", 128 * m, 128 * m + 128), r("loc", OFF + 128 * m, OFF + 128 * m + 128), 128)
            half_list = lambda m: ts(r("fo", 8 * m, 8 * m + 8), r("flx", 128 * m + 15, 128 * m + 128, st=16), cf(5), Op.subtract)
            half_row(0)
            quant("big", o, o + 128, "xt", 0, 512)
            y_of()
            half_list(0)
            half_row(1)
            pick("fin", 0, "big", o + S, "fo", 0, 8)
            half_list(1)
            y_put(t, 0)
            y_put(t, 1)
            pick("fin", 128, "big", o + S, "fo", 8, 16)

    oc = lambda m: ("y", T.oc[:, 512 * m:512 * m + 512], T.fin[:, 128 * m:128 * m + 128].bitcast(dt.uint8), [r("fin", 128 * m, 128 * m + 128)], [])
    dmas("dout", [oc(0)] +
         [("y", T.y[:, 256 * o:256 * o + 256], T.sy[:, STR * o + OFF:STR * o + STR], [r("sy", STR * o, STR * o + STR)], []) for o in (0, 1)] +
         [oc(1)] + [("s", T.osc[4 * k:4 * k + 4, :], T.fins[32 * k:32 * k + 4, :], [r("fins", 0, 256)], []) for k in range(4)])
    for sem in cnt:
        if known["g"].get(sem, 0) < cnt[sem]:
            g.wait_ge(T.sem[sem], cnt[sem])
